import numpy as np
import ml_dtypes


def mxq(x, axis, fmt="e4m3"):
    dtype, down = {"e4m3": (ml_dtypes.float8_e4m3fn, 7), "e5m2": (ml_dtypes.float8_e5m2, 14)}[fmt]
    v = np.moveaxis(np.asarray(x, np.float32).astype(ml_dtypes.bfloat16).astype(np.float64), axis, -1)
    blocks = v.reshape(v.shape[:-1] + (-1, 32))
    amax = np.abs(blocks).max(-1, keepdims=True)
    byte = np.maximum(np.where(amax > 0, np.frexp(amax)[1] - 1 + 127, 0) - down, 1)
    scale = np.exp2(byte - 127.0)
    codes = (blocks / scale).astype(np.float32).astype(dtype).astype(np.float64)
    return np.moveaxis((codes * scale).reshape(v.shape), -1, axis)


WIDE = False


def mx_kscale(k):
    if not WIDE:
        return np.ones(k)
    levels = np.array([10, -10, 5, -5, 0])
    if k % 512:
        return np.exp2(np.random.permutation(np.resize(levels, k // 32))).repeat(32)
    a = np.empty((k // 512, 16))
    for p in range(k // 512):
        a[p, :8] = np.random.permutation(np.resize(levels, 8))
        for g in range(8):
            far = levels[np.abs(levels - a[p, g]) >= 10]
            a[p, g + 8] = far[np.random.randint(len(far))]
    return np.exp2(a.ravel()).repeat(32)


def f64(x):
    return np.asarray(x).astype(np.float64)


def striped(idx):
    return np.tile(idx.reshape(-1, 16).T, (8, 1)).astype(np.uint16)


def unstriped(offs):
    return offs[:16].T.reshape(-1).astype(np.int64)


def pack_weight(w):
    k, n = w.shape
    w = f64(np.asarray(w, np.float32).astype(ml_dtypes.bfloat16)).reshape(k // 32, 32, n)
    amax = np.abs(w).max(1)
    byte = np.clip(np.where(amax > 0, np.frexp(amax)[1] - 1 + 127 - 7, 1), 1, 254)
    scaled = (w * np.exp2(127.0 - byte)[:, None, :]).reshape(k, n).astype(np.float32)
    words = np.ascontiguousarray(scaled.reshape(k // 512, 128, 4, n).transpose(0, 1, 3, 2)).astype(ml_dtypes.float8_e4m3fn).view(np.uint8)
    return words, np.ascontiguousarray(byte.astype(np.uint8).reshape(k // 512, 16, n))


def unpack_weight(words, scales):
    g, p, n, _ = words.shape
    vals = np.ascontiguousarray(words).view(ml_dtypes.float8_e4m3fn).astype(np.float64) * np.repeat(np.exp2(scales.astype(np.float64) - 127.0), 8, axis=1)[..., None]
    return vals.transpose(0, 1, 3, 2).reshape(g * 512, n)


def sigmoid(v):
    return 1.0 / (1.0 + np.exp(-np.maximum(v, -700.0)))


K, T, S, J = 1024, 2048, 512, 512
P = 2 ** 7


def setup_inputs():
    n = np.random.standard_normal
    s = mx_kscale(K)[:, None]
    packed_xT = pack_weight(n((K, T)) * s)
    return {
        "x_words": packed_xT[0],
        "x_scales": packed_xT[1],
        "hT": (n((K, J)) / np.sqrt(K) / s).astype(np.float32),
        "gain": (np.tile(np.random.uniform(0.5, 1.5, T), (P, 1))).astype(np.float32),
        "shift": (np.tile(0.5 * np.random.standard_normal(T), (P, 1))).astype(np.float32),
        "offs": striped(np.random.permutation(T)[:S]),
    }


def reference(x_words, x_scales, hT, gain, shift, offs):
    hTq = mxq(f64(hT), 0, "e4m3")
    xq = unpack_weight(x_words, x_scales)[:, unstriped(offs)]
    y = hTq.T @ xq
    g = f64(gain)[:1][:, unstriped(offs)]
    s_ = f64(shift)[:1][:, unstriped(offs)]
    return sigmoid(y * g + s_)

@@ -1,0 +1,173 @@
+from contextlib import ExitStack
+
+import concourse.mybir as mybir
+from concourse.masks import make_identity
+
+F32 = mybir.dt.float32
+BF16 = mybir.dt.bfloat16
+I32 = mybir.dt.int32
+U32 = mybir.dt.uint32
+U16 = mybir.dt.uint16
+U8 = mybir.dt.uint8
+FP8X4 = mybir.dt.float8_e4m3fn_x4
+SIGMOID = mybir.ActivationFunctionType.Sigmoid
+
+P = 128
+K, LABELS, PICKED, DOCS = 1024, 2048, 512, 512
+PASSES = 2
+FLOPS = 2 * K * PICKED * DOCS
+BYTES = K * LABELS + K // 32 * LABELS + 4 * K * DOCS + 2 * 4 * LABELS + 2 * PICKED + 4 * DOCS * PICKED
+GAIN_ROW, SHIFT_ROW = 16, 80
+CHUNKS = [(0, 256, 160), (256, 256, 256)]
+BANKS = [(0, 2), (2, 2)]
+
+
+def tile_picked_zplatt_sig_p_kernel(tc, x_words, x_scales, hT, gain, shift, offs, out):
+    nc = tc.nc
+    with ExitStack() as ctx:
+        keep = ctx.enter_context(tc.tile_pool(name="keep", bufs=1))
+        psum = ctx.enter_context(tc.psum_pool(name="psum", bufs=1))
+
+        def sb(shape, dtype, name):
+            return keep.tile(shape, dtype, name=name, align_bytes=64)
+
+        def shared(shape, dtype, name, tag):
+            return keep.tile(shape, dtype, name=name, tag=tag, align_bytes=64)
+
+        offsets = sb([P, PICKED // 16], U16, "offsets")
+        scale_window = sb([P, LABELS], U8, "scale_window")
+        row_window = sb([P, LABELS], F32, "row_window")
+        h_rows = [hT[512 * o : 512 * (o + 1), :].rearrange("(p j) t -> p j t", j=4) for o in range(PASSES)]
+        warm_in = shared([P, 1], F32, "warm_in", "slot_x1")
+        warm_out = shared([P, 1], F32, "warm_out", "slot_h0")
+
+        nc.gpsimd.memset(scale_window[:].bitcast(I32), 0)
+        nc.vector.memset(row_window[:], 0.0)
+        nc.vector.memset(warm_in[:], 0.0)
+        nc.scalar.activation(warm_out[:], warm_in[:], SIGMOID)
+
+        word_window = [
+            shared([P, LABELS], I32, "word_window0", "slot_x0"),
+            shared([P, LABELS], I32, "word_window1", "slot_x1"),
+        ]
+        h0_raw = shared([P, 4, DOCS], F32, "h0_raw", "slot_h0")
+
+        def load_words(o):
+            nc.sync.dma_start(word_window[o][:], x_words[o].rearrange("p n t -> p (n t)").bitcast(I32))
+
+        nc.sync.dma_start(offsets[:], offs)
+        load_words(0)
+        for q in range(4):
+            nc.sync.dma_start(
+                scale_window[32 * q : 32 * q + 8, :].bitcast(I32),
+                x_scales[:, 4 * q : 4 * q + 4, :].bitcast(I32),
+            )
+        nc.sync.dma_start(row_window[GAIN_ROW : GAIN_ROW + 1, :], gain[0:1, :])
+        nc.sync.dma_start(row_window[SHIFT_ROW : SHIFT_ROW + 1, :], shift[0:1, :])
+        nc.sync.dma_start(h0_raw[:], h_rows[0])
+        load_words(1)
+        identity = sb([P, P], F32, "identity")
+        make_identity(nc, identity[:])
+
+        sums = [psum.tile([P, 512], F32, name="sums%d" % b) for b in range(4)]
+        turned = [psum.tile([P, 512], F32, name="turned%d" % b) for b in range(4)]
+
+        picked_rows = sb([P, PICKED], F32, "picked_rows")
+        nc.vector.tensor_copy(picked_rows[:], row_window[:].indirect(offsets[:]))
+        for b in range(4):
+            nc.tensor.transpose(turned[3][:, P * b : P * (b + 1)], picked_rows[:, P * b : P * (b + 1)], identity[:])
+        x_codes = [
+            sb([P, PICKED], U32, "x_codes0"),
+            sb([P, PICKED], U32, "x_codes1"),
+        ]
+        x_bytes = sb([P, PICKED], U8, "x_bytes")
+        nc.vector.tensor_copy(x_codes[0][:], word_window[0][:].bitcast(U32).indirect(offsets[:]))
+        h1_all = shared([P, 4 * DOCS], F32, "h1_all", "slot_x0")
+        h1_raw = [h1_all[:, 4 * t0 : 4 * (t0 + w)].rearrange("p (j t) -> p j t", j=4) for t0, w, cut in CHUNKS]
+        for c, (t0, w, cut) in enumerate(CHUNKS):
+            nc.sync.dma_start(h1_raw[c], h_rows[1][:, :, t0 : t0 + w])
+        nc.vector.tensor_copy(x_bytes[:], scale_window[:].indirect(offsets[:]))
+
+        def interleave(copy, grouped, raw):
+            copy(grouped.rearrange("p (c i) j -> p c j i", i=4), raw.rearrange("p j (c i) -> p c j i", i=4))
+
+        def cast(raw, cut, name, tag):
+            grouped = shared([P, 256, 4], BF16, name + "_grouped", tag)
+            if cut > 0:
+                interleave(nc.vector.tensor_copy, grouped[:, 0:cut, :], raw[:, :, 0:cut])
+            if cut < 256:
+                interleave(nc.scalar.copy, grouped[:, cut:256, :], raw[:, :, cut:256])
+            return grouped
+
+        def quantise(grouped, name, tag):
+            codes = shared([P, 256], U32, name + "_codes", tag)
+            scales = sb([P, 256], U8, name + "_scales")
+            nc.vector.quantize_mx(
+                out=codes[:].bitcast(FP8X4), scales=scales[:], in_=grouped[:].rearrange("p t j -> p (t j)")
+            )
+            return codes, scales
+
+        h0_grouped = [cast(h0_raw[:, :, 256 * c : 256 * (c + 1)], 0, "h0_%d" % c, "slot_g0%d" % c) for c in range(2)]
+        platt = shared([P, 4, 2], F32, "platt", "slot_h0")
+        nc.scalar.copy(
+            platt[:], turned[3][:].rearrange("p (b r) -> p b r", b=4)[:, :, GAIN_ROW :: SHIFT_ROW - GAIN_ROW]
+        )
+
+        def region(c, b):
+            w = CHUNKS[c][1]
+            bank, per_bank = BANKS[c]
+            i = b % per_bank
+            return sums[bank + b // per_bank][:, i * w : (i + 1) * w], i == 0, i == per_bank - 1
+
+        def multiply(o, c, codes, scales):
+            for b in range(4):
+                labels = slice(P * b, P * (b + 1))
+                target, first, last = region(c, b)
+                nc.tensor.matmul_mx(
+                    out=target,
+                    lhsT=x_codes[o][:, labels].bitcast(FP8X4),
+                    lhsT_scale=x_bytes[4 * o :, labels],
+                    rhs=codes[:].bitcast(FP8X4),
+                    rhs_scale=scales[:],
+                    start=first and o == 0,
+                    stop=last and o == 1,
+                )
+
+        multiply(0, 0, *quantise(h0_grouped[0], "h0_0", "slot_c00"))
+        nc.vector.tensor_copy(x_codes[1][:], word_window[1][:].bitcast(U32).indirect(offsets[:]))
+        multiply(1, 0, *quantise(cast(h1_raw[0], CHUNKS[0][2], "h1_0", "slot_g10"), "h1_0", "slot_c10"))
+        multiply(0, 1, *quantise(h0_grouped[1], "h0_1", "slot_g10"))
+        multiply(1, 1, *quantise(cast(h1_raw[1], CHUNKS[1][2], "h1_1", "slot_g01"), "h1_1", "slot_c11"))
+
+        for c, (t0, w, cut) in enumerate(CHUNKS):
+            probs = sb([P, 4, w], F32, "probs%d" % c)
+            groups = [region(c, b)[0] for b in range(4)]
+            for b in range(4):
+                nc.scalar.activation(probs[:, b, :], groups[b], SIGMOID, bias=platt[:, b, 1:2], scale=platt[:, b, 0:1])
+            for half in range(2):
+                cols = slice(256 * half, 256 * (half + 1))
+                if 2 * c + half < 3:
+                    bank = turned[2 * c + half]
+                    for i in range(2):
+                        for s in range(2):
+                            nc.tensor.transpose(
+                                bank[:, 256 * s + P * i : 256 * s + P * (i + 1)],
+                                probs[:, 2 * half + i, P * s : P * (s + 1)],
+                                identity[:],
+                            )
+                    result = sb([P, 2, 256], F32, "result%d" % (2 * c + half))
+                    nc.vector.tensor_copy(result[:].rearrange("p s j -> p (s j)"), bank[:])
+                    nc.sync.dma_start(out[t0 : t0 + w, cols].rearrange("(s p) j -> p s j", s=2), result[:])
+                else:
+                    banks = [turned[3], turned[0]]
+                    for i in range(2):
+                        for s in range(2):
+                            nc.tensor.transpose(
+                                banks[s][:, P * i : P * (i + 1)],
+                                probs[:, 2 * half + i, P * s : P * (s + 1)],
+                                identity[:],
+                            )
+                    for s, (copy, queue) in enumerate([(nc.vector.tensor_copy, nc.sync), (nc.scalar.copy, nc.scalar)]):
+                        result = sb([P, 256], F32, "last%d" % s)
+                        copy(result[:], banks[s][:, 0:256])
+                        queue.dma_start(out[t0 + P * s : t0 + P * (s + 1), cols], result[:])

@@ -18,8 +18,8 @@ PASSES = 2
 FLOPS = 2 * K * PICKED * DOCS
 BYTES = K * LABELS + K // 32 * LABELS + 4 * K * DOCS + 2 * 4 * LABELS + 2 * PICKED + 4 * DOCS * PICKED
 GAIN_ROW, SHIFT_ROW = 16, 80
-CHUNKS = [(0, 256, 160), (256, 256, 256)]
-BANKS = [(0, 2), (2, 2)]
+CHUNKS = [(0, 256), (256, 128), (384, 128)]
+BANKS = [(0, 2), (2, 4), (3, 4)]
 
 
 def tile_picked_zplatt_sig_p_kernel(tc, x_words, x_scales, hT, gain, shift, offs, out):
@@ -28,35 +28,34 @@ def tile_picked_zplatt_sig_p_kernel(tc, x_words, x_scales, hT, gain, shift, offs
         keep = ctx.enter_context(tc.tile_pool(name="keep", bufs=1))
         psum = ctx.enter_context(tc.psum_pool(name="psum", bufs=1))
 
-        def sb(shape, dtype, name):
-            return keep.tile(shape, dtype, name=name, align_bytes=64)
-
-        def shared(shape, dtype, name, tag):
-            return keep.tile(shape, dtype, name=name, tag=tag, align_bytes=64)
+        def sb(shape, dtype, name, slot=None):
+            return keep.tile(shape, dtype, name=name, tag=slot or name, align_bytes=64)
 
         offsets = sb([P, PICKED // 16], U16, "offsets")
         scale_window = sb([P, LABELS], U8, "scale_window")
-        row_window = sb([P, LABELS], F32, "row_window")
+        row_window = sb([P, LABELS], F32, "row_window", "slot_rows")
         h_rows = [hT[512 * o : 512 * (o + 1), :].rearrange("(p j) t -> p j t", j=4) for o in range(PASSES)]
-        warm_in = shared([P, 1], F32, "warm_in", "slot_x1")
-        warm_out = shared([P, 1], F32, "warm_out", "slot_h0")
+        warm_in = sb([P, 1], F32, "warm_in", "slot_h1a")
+        warm_out = sb([P, 1], F32, "warm_out", "slot_h0")
 
         nc.gpsimd.memset(scale_window[:].bitcast(I32), 0)
         nc.vector.memset(row_window[:], 0.0)
         nc.vector.memset(warm_in[:], 0.0)
         nc.scalar.activation(warm_out[:], warm_in[:], SIGMOID)
 
-        word_window = [
-            shared([P, LABELS], I32, "word_window0", "slot_x0"),
-            shared([P, LABELS], I32, "word_window1", "slot_x1"),
-        ]
-        h0_raw = shared([P, 4, DOCS], F32, "h0_raw", "slot_h0")
+        def load_words(o, slot):
+            window = sb([P, LABELS], I32, "word_window%d" % o, slot)
+            nc.sync.dma_start(window[:], x_words[o].rearrange("p n t -> p (n t)").bitcast(I32))
+            return window
 
-        def load_words(o):
-            nc.sync.dma_start(word_window[o][:], x_words[o].rearrange("p n t -> p (n t)").bitcast(I32))
+        def load_docs(o, t0, width, slot):
+            raw = sb([P, 4, width], F32, "h%d_raw%d" % (o, t0), slot)
+            nc.sync.dma_start(raw[:], h_rows[o][:, :, t0 : t0 + width])
+            return raw
 
+        identity = sb([P, P], F32, "identity")
         nc.sync.dma_start(offsets[:], offs)
-        load_words(0)
+        window0 = load_words(0, "slot_x0")
         for q in range(4):
             nc.sync.dma_start(
                 scale_window[32 * q : 32 * q + 8, :].bitcast(I32),
@@ -64,110 +63,116 @@ def tile_picked_zplatt_sig_p_kernel(tc, x_words, x_scales, hT, gain, shift, offs
             )
         nc.sync.dma_start(row_window[GAIN_ROW : GAIN_ROW + 1, :], gain[0:1, :])
         nc.sync.dma_start(row_window[SHIFT_ROW : SHIFT_ROW + 1, :], shift[0:1, :])
-        nc.sync.dma_start(h0_raw[:], h_rows[0])
-        load_words(1)
-        identity = sb([P, P], F32, "identity")
+        h0_raw = load_docs(0, 0, DOCS, "slot_h0")
+        h1_raw = [load_docs(1, 0, 256, "slot_h1a")[:]]
         make_identity(nc, identity[:])
 
         sums = [psum.tile([P, 512], F32, name="sums%d" % b) for b in range(4)]
         turned = [psum.tile([P, 512], F32, name="turned%d" % b) for b in range(4)]
 
+        x0_codes = sb([P, PICKED], U32, "x0_codes")
+        nc.vector.tensor_copy(x0_codes[:], window0[:].bitcast(U32).indirect(offsets[:]))
+        window1 = load_words(1, "slot_x0")
+
         picked_rows = sb([P, PICKED], F32, "picked_rows")
         nc.vector.tensor_copy(picked_rows[:], row_window[:].indirect(offsets[:]))
+        h1_late = sb([P, 1024], F32, "h1_late", "slot_rows")
+        for c in (1, 2):
+            h1_raw.append(h1_late[:, 512 * (c - 1) : 512 * c].rearrange("p (j t) -> p j t", j=4))
+            nc.sync.dma_start(h1_raw[c], h_rows[1][:, :, CHUNKS[c][0] : CHUNKS[c][0] + P])
         for b in range(4):
             nc.tensor.transpose(turned[3][:, P * b : P * (b + 1)], picked_rows[:, P * b : P * (b + 1)], identity[:])
-        x_codes = [
-            sb([P, PICKED], U32, "x_codes0"),
-            sb([P, PICKED], U32, "x_codes1"),
-        ]
         x_bytes = sb([P, PICKED], U8, "x_bytes")
-        nc.vector.tensor_copy(x_codes[0][:], word_window[0][:].bitcast(U32).indirect(offsets[:]))
-        h1_all = shared([P, 4 * DOCS], F32, "h1_all", "slot_x0")
-        h1_raw = [h1_all[:, 4 * t0 : 4 * (t0 + w)].rearrange("p (j t) -> p j t", j=4) for t0, w, cut in CHUNKS]
-        for c, (t0, w, cut) in enumerate(CHUNKS):
-            nc.sync.dma_start(h1_raw[c], h_rows[1][:, :, t0 : t0 + w])
         nc.vector.tensor_copy(x_bytes[:], scale_window[:].indirect(offsets[:]))
 
-        def interleave(copy, grouped, raw):
-            copy(grouped.rearrange("p (c i) j -> p c j i", i=4), raw.rearrange("p j (c i) -> p c j i", i=4))
-
-        def cast(raw, cut, name, tag):
-            grouped = shared([P, 256, 4], BF16, name + "_grouped", tag)
-            if cut > 0:
-                interleave(nc.vector.tensor_copy, grouped[:, 0:cut, :], raw[:, :, 0:cut])
-            if cut < 256:
-                interleave(nc.scalar.copy, grouped[:, cut:256, :], raw[:, :, cut:256])
+        def cast(copy, raw, name, slot=None):
+            width = raw.shape[2]
+            grouped = sb([P, width, 4], BF16, name + "_grouped", slot)
+            copy(grouped[:].rearrange("p (c i) j -> p c j i", i=4), raw.rearrange("p j (c i) -> p c j i", i=4))
             return grouped
 
-        def quantise(grouped, name, tag):
-            codes = shared([P, 256], U32, name + "_codes", tag)
-            scales = sb([P, 256], U8, name + "_scales")
+        def quantise(grouped, name):
+            width = grouped.shape[1]
+            codes = sb([P, width], U32, name + "_codes")
+            scales = sb([P, width], U8, name + "_scales")
             nc.vector.quantize_mx(
                 out=codes[:].bitcast(FP8X4), scales=scales[:], in_=grouped[:].rearrange("p t j -> p (t j)")
             )
-            return codes, scales
-
-        h0_grouped = [cast(h0_raw[:, :, 256 * c : 256 * (c + 1)], 0, "h0_%d" % c, "slot_g0%d" % c) for c in range(2)]
-        platt = shared([P, 4, 2], F32, "platt", "slot_h0")
-        nc.scalar.copy(
-            platt[:], turned[3][:].rearrange("p (b r) -> p b r", b=4)[:, :, GAIN_ROW :: SHIFT_ROW - GAIN_ROW]
-        )
+            return codes[:], scales[:]
 
         def region(c, b):
-            w = CHUNKS[c][1]
+            width = CHUNKS[c][1]
             bank, per_bank = BANKS[c]
             i = b % per_bank
-            return sums[bank + b // per_bank][:, i * w : (i + 1) * w], i == 0, i == per_bank - 1
+            return sums[bank + b // per_bank][:, i * width : (i + 1) * width], i == 0, i == per_bank - 1
 
-        def multiply(o, c, codes, scales):
+        def multiply(o, c, label_codes, codes, scales):
             for b in range(4):
-                labels = slice(P * b, P * (b + 1))
                 target, first, last = region(c, b)
                 nc.tensor.matmul_mx(
                     out=target,
-                    lhsT=x_codes[o][:, labels].bitcast(FP8X4),
-                    lhsT_scale=x_bytes[4 * o :, labels],
-                    rhs=codes[:].bitcast(FP8X4),
-                    rhs_scale=scales[:],
+                    lhsT=label_codes[b].bitcast(FP8X4),
+                    lhsT_scale=x_bytes[4 * o :, P * b : P * (b + 1)],
+                    rhs=codes.bitcast(FP8X4),
+                    rhs_scale=scales,
                     start=first and o == 0,
                     stop=last and o == 1,
                 )
 
-        multiply(0, 0, *quantise(h0_grouped[0], "h0_0", "slot_c00"))
-        nc.vector.tensor_copy(x_codes[1][:], word_window[1][:].bitcast(U32).indirect(offsets[:]))
-        multiply(1, 0, *quantise(cast(h1_raw[0], CHUNKS[0][2], "h1_0", "slot_g10"), "h1_0", "slot_c10"))
-        multiply(0, 1, *quantise(h0_grouped[1], "h0_1", "slot_g10"))
-        multiply(1, 1, *quantise(cast(h1_raw[1], CHUNKS[1][2], "h1_1", "slot_g01"), "h1_1", "slot_c11"))
+        h0_grouped = [cast(nc.scalar.copy, h0_raw[:, :, 256 * i : 256 * (i + 1)], "h0_%d" % i) for i in range(2)]
+        platt = sb([P, 4, 2], F32, "platt", "slot_h0")
+        nc.scalar.copy(
+            platt[:], turned[3][:].rearrange("p (b r) -> p b r", b=4)[:, :, GAIN_ROW :: SHIFT_ROW - GAIN_ROW]
+        )
 
-        for c, (t0, w, cut) in enumerate(CHUNKS):
-            probs = sb([P, 4, w], F32, "probs%d" % c)
-            groups = [region(c, b)[0] for b in range(4)]
+        x0_blocks = [x0_codes[:, P * b : P * (b + 1)] for b in range(4)]
+        multiply(0, 0, x0_blocks, *quantise(h0_grouped[0], "h0_0"))
+        h1_first = quantise(cast(nc.vector.tensor_copy, h1_raw[0], "h1_0"), "h1_0")
+        codes, scales = quantise(h0_grouped[1], "h0_1")
+        for c in (1, 2):
+            docs = slice(P * (c - 1), P * c)
+            multiply(0, c, x0_blocks, codes[:, docs], scales[:, docs])
+
+        x1_blocks = []
+        for half in range(2):
+            x1_codes = sb([P, 256], U32, "x1_codes%d" % half)
+            nc.vector.tensor_copy(
+                x1_codes[:], window1[:].bitcast(U32).indirect(offsets[:, 16 * half : 16 * (half + 1)])
+            )
+            x1_blocks.extend([x1_codes[:, 0:P], x1_codes[:, P : 2 * P]])
+        multiply(1, 0, x1_blocks, *h1_first)
+        for c in (1, 2):
+            grouped = cast(nc.vector.tensor_copy, h1_raw[c], "h1_%d" % c, "slot_x0")
+            multiply(1, c, x1_blocks, *quantise(grouped, "h1_%d" % c))
+
+        probs = []
+        for c, (t0, width) in enumerate(CHUNKS):
+            probs.append(sb([P, 4, width], F32, "probs%d" % c))
             for b in range(4):
-                nc.scalar.activation(probs[:, b, :], groups[b], SIGMOID, bias=platt[:, b, 1:2], scale=platt[:, b, 0:1])
-            for half in range(2):
-                cols = slice(256 * half, 256 * (half + 1))
-                if 2 * c + half < 3:
-                    bank = turned[2 * c + half]
-                    for i in range(2):
-                        for s in range(2):
-                            nc.tensor.transpose(
-                                bank[:, 256 * s + P * i : 256 * s + P * (i + 1)],
-                                probs[:, 2 * half + i, P * s : P * (s + 1)],
-                                identity[:],
-                            )
-                    result = sb([P, 2, 256], F32, "result%d" % (2 * c + half))
-                    nc.vector.tensor_copy(result[:].rearrange("p s j -> p (s j)"), bank[:])
-                    nc.sync.dma_start(out[t0 : t0 + w, cols].rearrange("(s p) j -> p s j", s=2), result[:])
-                else:
-                    banks = [turned[3], turned[0]]
-                    for i in range(2):
-                        for s in range(2):
-                            nc.tensor.transpose(
-                                banks[s][:, P * i : P * (i + 1)],
-                                probs[:, 2 * half + i, P * s : P * (s + 1)],
-                                identity[:],
-                            )
-                    for s, (copy, queue) in enumerate([(nc.vector.tensor_copy, nc.sync), (nc.scalar.copy, nc.scalar)]):
-                        result = sb([P, 256], F32, "last%d" % s)
-                        copy(result[:], banks[s][:, 0:256])
-                        queue.dma_start(out[t0 + P * s : t0 + P * (s + 1), cols], result[:])
+                nc.scalar.activation(
+                    probs[c][:, b, :], region(c, b)[0], SIGMOID, bias=platt[:, b, 1:2], scale=platt[:, b, 0:1]
+                )
+
+        def put_out(c, b0, blocks, bank, copy, queue):
+            t0, width = CHUNKS[c]
+            groups = width // P
+            cols = P * blocks
+            for i in range(blocks):
+                for s in range(groups):
+                    nc.tensor.transpose(
+                        bank[:, cols * s + P * i : cols * s + P * (i + 1)],
+                        probs[c][:, b0 + i, P * s : P * (s + 1)],
+                        identity[:],
+                    )
+            result = sb([P, groups, cols], F32, "result%d_%d" % (c, b0))
+            copy(result[:].rearrange("p s j -> p (s j)"), bank[:, 0 : groups * cols])
+            queue.dma_start(
+                out[t0 : t0 + width, P * b0 : P * b0 + cols].rearrange("(s p) j -> p s j", s=groups), result[:]
+            )
+
+        put_out(0, 0, 2, turned[0], nc.vector.tensor_copy, nc.sync)
+        put_out(0, 2, 2, turned[1], nc.vector.tensor_copy, nc.sync)
+        put_out(1, 0, 4, turned[2], nc.vector.tensor_copy, nc.sync)
+        put_out(2, 0, 2, turned[3], nc.scalar.copy, nc.scalar)
+        put_out(2, 2, 1, turned[0], nc.vector.tensor_copy, nc.sync)
+        put_out(2, 3, 1, turned[1], nc.scalar.copy, nc.scalar)

@@ -17,9 +17,7 @@ K, LABELS, PICKED, DOCS = 1024, 2048, 512, 512
 PASSES = 2
 FLOPS = 2 * K * PICKED * DOCS
 BYTES = K * LABELS + K // 32 * LABELS + 4 * K * DOCS + 2 * 4 * LABELS + 2 * PICKED + 4 * DOCS * PICKED
-GAIN_ROW, SHIFT_ROW = 16, 80
-CHUNKS = [(0, 256), (256, 128), (384, 128)]
-BANKS = [(0, 2), (2, 4), (3, 4)]
+GAIN_ROW = 126
 
 
 def tile_picked_zplatt_sig_p_kernel(tc, x_words, x_scales, hT, gain, shift, offs, out):
@@ -33,62 +31,63 @@ def tile_picked_zplatt_sig_p_kernel(tc, x_words, x_scales, hT, gain, shift, offs
 
         offsets = sb([P, PICKED // 16], U16, "offsets")
         scale_window = sb([P, LABELS], U8, "scale_window")
-        row_window = sb([P, LABELS], F32, "row_window", "slot_rows")
+        row_window = sb([P, LABELS], F32, "row_window")
         h_rows = [hT[512 * o : 512 * (o + 1), :].rearrange("(p j) t -> p j t", j=4) for o in range(PASSES)]
-        warm_in = sb([P, 1], F32, "warm_in", "slot_h1a")
-        warm_out = sb([P, 1], F32, "warm_out", "slot_h0")
+        warm_in = sb([P, 1], F32, "warm_in")
+        warm_out = sb([P, 1], F32, "warm_out")
+        identity = sb([P, P], F32, "identity")
 
-        nc.gpsimd.memset(scale_window[:].bitcast(I32), 0)
-        nc.vector.memset(row_window[:], 0.0)
-        nc.vector.memset(warm_in[:], 0.0)
+        nc.gpsimd.memset(warm_in[:], 0.0)
+        nc.vector.memset(scale_window[:].bitcast(I32)[:, 0:256], 0)
+        nc.gpsimd.memset(scale_window[:].bitcast(I32)[:, 256:512], 0)
         nc.scalar.activation(warm_out[:], warm_in[:], SIGMOID)
+        nc.vector.memset(row_window[0:GAIN_ROW, :], 0.0)
+        make_identity(nc, identity[:])
 
-        def load_words(o, slot):
-            window = sb([P, LABELS], I32, "word_window%d" % o, slot)
+        def load_words(o):
+            window = sb([P, LABELS], I32, "word_window%d" % o)
             nc.sync.dma_start(window[:], x_words[o].rearrange("p n t -> p (n t)").bitcast(I32))
             return window
 
-        def load_docs(o, t0, width, slot):
-            raw = sb([P, 4, width], F32, "h%d_raw%d" % (o, t0), slot)
+        def load_docs(o, t0, width):
+            raw = sb([P, 4, width], F32, "h%d_raw%d" % (o, t0))
             nc.sync.dma_start(raw[:], h_rows[o][:, :, t0 : t0 + width])
             return raw
 
-        identity = sb([P, P], F32, "identity")
         nc.sync.dma_start(offsets[:], offs)
-        window0 = load_words(0, "slot_x0")
+        nc.sync.dma_start(row_window[GAIN_ROW : GAIN_ROW + 1, :], gain[0:1, :])
+        nc.sync.dma_start(row_window[GAIN_ROW + 1 : GAIN_ROW + 2, :], shift[0:1, :])
+        window0 = load_words(0)
         for q in range(4):
             nc.sync.dma_start(
                 scale_window[32 * q : 32 * q + 8, :].bitcast(I32),
                 x_scales[:, 4 * q : 4 * q + 4, :].bitcast(I32),
             )
-        nc.sync.dma_start(row_window[GAIN_ROW : GAIN_ROW + 1, :], gain[0:1, :])
-        nc.sync.dma_start(row_window[SHIFT_ROW : SHIFT_ROW + 1, :], shift[0:1, :])
-        h0_raw = load_docs(0, 0, DOCS, "slot_h0")
-        h1_raw = [load_docs(1, 0, 256, "slot_h1a")[:]]
-        make_identity(nc, identity[:])
+        raw_ab0 = load_docs(0, 0, 256)
+        window1 = load_words(1)
+        raw_a1 = load_docs(1, 0, P)
+        raw_b1 = load_docs(1, P, P)
+        raw_c0 = load_docs(0, 2 * P, P)
+        raw_c1 = load_docs(1, 2 * P, P)
+        raw_d0 = load_docs(0, 3 * P, P)
+        raw_d1 = load_docs(1, 3 * P, P)
 
-        sums = [psum.tile([P, 512], F32, name="sums%d" % b) for b in range(4)]
-        turned = [psum.tile([P, 512], F32, name="turned%d" % b) for b in range(4)]
-
-        x0_codes = sb([P, PICKED], U32, "x0_codes")
-        nc.vector.tensor_copy(x0_codes[:], window0[:].bitcast(U32).indirect(offsets[:]))
-        window1 = load_words(1, "slot_x0")
+        sums = [psum.tile([P, 512], F32, name="sums%d" % b) for b in range(5)]
+        turned = [psum.tile([P, 512], F32, name="turned%d" % b) for b in range(3)]
 
         picked_rows = sb([P, PICKED], F32, "picked_rows")
         nc.vector.tensor_copy(picked_rows[:], row_window[:].indirect(offsets[:]))
-        h1_late = sb([P, 1024], F32, "h1_late", "slot_rows")
-        for c in (1, 2):
-            h1_raw.append(h1_late[:, 512 * (c - 1) : 512 * c].rearrange("p (j t) -> p j t", j=4))
-            nc.sync.dma_start(h1_raw[c], h_rows[1][:, :, CHUNKS[c][0] : CHUNKS[c][0] + P])
-        for b in range(4):
-            nc.tensor.transpose(turned[3][:, P * b : P * (b + 1)], picked_rows[:, P * b : P * (b + 1)], identity[:])
+        x0_codes = sb([P, PICKED], U32, "x0_codes")
+        nc.vector.tensor_copy(x0_codes[:], window0[:].bitcast(U32).indirect(offsets[:]))
         x_bytes = sb([P, PICKED], U8, "x_bytes")
         nc.vector.tensor_copy(x_bytes[:], scale_window[:].indirect(offsets[:]))
+        for b in range(4):
+            nc.tensor.transpose(turned[2][:, P * b : P * (b + 1)], picked_rows[:, P * b : P * (b + 1)], identity[:])
 
-        def cast(copy, raw, name, slot=None):
+        def cast(copy, raw, name):
             width = raw.shape[2]
-            grouped = sb([P, width, 4], BF16, name + "_grouped", slot)
-            copy(grouped[:].rearrange("p (c i) j -> p c j i", i=4), raw.rearrange("p j (c i) -> p c j i", i=4))
+            grouped = sb([P, width, 4], BF16, name + "_grouped")
+            copy(grouped[:].rearrange("p (c i) j -> p c j i", i=4), raw[:].rearrange("p j (c i) -> p c j i", i=4))
             return grouped
 
         def quantise(grouped, name):
@@ -101,10 +100,9 @@ def tile_picked_zplatt_sig_p_kernel(tc, x_words, x_scales, hT, gain, shift, offs
             return codes[:], scales[:]
 
         def region(c, b):
-            width = CHUNKS[c][1]
-            bank, per_bank = BANKS[c]
-            i = b % per_bank
-            return sums[bank + b // per_bank][:, i * width : (i + 1) * width], i == 0, i == per_bank - 1
+            if c < 3:
+                return sums[c][:, P * b : P * (b + 1)], b == 0, b == 3
+            return sums[3 + b // 2][:, P * (b % 2) : P * (b % 2 + 1)], b % 2 == 0, b % 2 == 1
 
         def multiply(o, c, label_codes, codes, scales):
             for b in range(4):
@@ -119,60 +117,61 @@ def tile_picked_zplatt_sig_p_kernel(tc, x_words, x_scales, hT, gain, shift, offs
                     stop=last and o == 1,
                 )
 
-        h0_grouped = [cast(nc.scalar.copy, h0_raw[:, :, 256 * i : 256 * (i + 1)], "h0_%d" % i) for i in range(2)]
-        platt = sb([P, 4, 2], F32, "platt", "slot_h0")
-        nc.scalar.copy(
-            platt[:], turned[3][:].rearrange("p (b r) -> p b r", b=4)[:, :, GAIN_ROW :: SHIFT_ROW - GAIN_ROW]
-        )
+        grouped_ab0 = cast(nc.scalar.copy, raw_ab0, "ab0")
+        platt = sb([P, 4, 2], F32, "platt")
+        nc.scalar.copy(platt[:], turned[2][:].rearrange("p (b r) -> p b r", b=4)[:, :, GAIN_ROW : GAIN_ROW + 2])
+        codes_ab0, scales_ab0 = quantise(grouped_ab0, "ab0")
 
         x0_blocks = [x0_codes[:, P * b : P * (b + 1)] for b in range(4)]
-        multiply(0, 0, x0_blocks, *quantise(h0_grouped[0], "h0_0"))
-        h1_first = quantise(cast(nc.vector.tensor_copy, h1_raw[0], "h1_0"), "h1_0")
-        codes, scales = quantise(h0_grouped[1], "h0_1")
-        for c in (1, 2):
-            docs = slice(P * (c - 1), P * c)
-            multiply(0, c, x0_blocks, codes[:, docs], scales[:, docs])
+        for c in range(2):
+            docs = slice(P * c, P * (c + 1))
+            multiply(0, c, x0_blocks, codes_ab0[:, docs], scales_ab0[:, docs])
 
-        x1_blocks = []
-        for half in range(2):
-            x1_codes = sb([P, 256], U32, "x1_codes%d" % half)
-            nc.vector.tensor_copy(
-                x1_codes[:], window1[:].bitcast(U32).indirect(offsets[:, 16 * half : 16 * (half + 1)])
-            )
-            x1_blocks.extend([x1_codes[:, 0:P], x1_codes[:, P : 2 * P]])
-        multiply(1, 0, x1_blocks, *h1_first)
-        for c in (1, 2):
-            grouped = cast(nc.vector.tensor_copy, h1_raw[c], "h1_%d" % c, "slot_x0")
-            multiply(1, c, x1_blocks, *quantise(grouped, "h1_%d" % c))
+        x1_codes = sb([P, PICKED], U32, "x1_codes")
+        nc.vector.tensor_copy(x1_codes[:], window1[:].bitcast(U32).indirect(offsets[:]))
+        x1_blocks = [x1_codes[:, P * b : P * (b + 1)] for b in range(4)]
 
-        probs = []
-        for c, (t0, width) in enumerate(CHUNKS):
-            probs.append(sb([P, 4, width], F32, "probs%d" % c))
+        probs = [sb([P, 4, P], F32, "probs%d" % c) for c in range(4)]
+
+        def squash(c):
             for b in range(4):
                 nc.scalar.activation(
                     probs[c][:, b, :], region(c, b)[0], SIGMOID, bias=platt[:, b, 1:2], scale=platt[:, b, 0:1]
                 )
 
-        def put_out(c, b0, blocks, bank, copy, queue):
-            t0, width = CHUNKS[c]
-            groups = width // P
-            cols = P * blocks
+        def turn(c, b0, blocks, bank):
             for i in range(blocks):
-                for s in range(groups):
-                    nc.tensor.transpose(
-                        bank[:, cols * s + P * i : cols * s + P * (i + 1)],
-                        probs[c][:, b0 + i, P * s : P * (s + 1)],
-                        identity[:],
-                    )
-            result = sb([P, groups, cols], F32, "result%d_%d" % (c, b0))
-            copy(result[:].rearrange("p s j -> p (s j)"), bank[:, 0 : groups * cols])
-            queue.dma_start(
-                out[t0 : t0 + width, P * b0 : P * b0 + cols].rearrange("(s p) j -> p s j", s=groups), result[:]
-            )
+                nc.tensor.transpose(bank[:, P * i : P * (i + 1)], probs[c][:, b0 + i, :], identity[:])
 
-        put_out(0, 0, 2, turned[0], nc.vector.tensor_copy, nc.sync)
-        put_out(0, 2, 2, turned[1], nc.vector.tensor_copy, nc.sync)
-        put_out(1, 0, 4, turned[2], nc.vector.tensor_copy, nc.sync)
-        put_out(2, 0, 2, turned[3], nc.scalar.copy, nc.scalar)
-        put_out(2, 2, 1, turned[0], nc.vector.tensor_copy, nc.sync)
-        put_out(2, 3, 1, turned[1], nc.scalar.copy, nc.scalar)
+        def put_out(c, b0, blocks, bank, copy, queue):
+            cols = P * blocks
+            result = sb([P, cols], F32, "result%d_%d" % (c, b0))
+            copy(result[:], bank[:, 0:cols])
+            queue.dma_start(out[P * c : P * (c + 1), P * b0 : P * b0 + cols], result[:])
+
+        grouped_a1 = cast(nc.scalar.copy, raw_a1, "a1")
+        grouped_b1 = cast(nc.scalar.copy, raw_b1, "b1")
+        multiply(1, 0, x1_blocks, *quantise(grouped_a1, "a1"))
+        grouped_c0 = cast(nc.vector.tensor_copy, raw_c0, "c0")
+        multiply(1, 1, x1_blocks, *quantise(grouped_b1, "b1"))
+        squash(0)
+        grouped_c1 = cast(nc.vector.tensor_copy, raw_c1, "c1")
+        multiply(0, 2, x0_blocks, *quantise(grouped_c0, "c0"))
+        turn(0, 0, 4, turned[0])
+        squash(1)
+        multiply(1, 2, x1_blocks, *quantise(grouped_c1, "c1"))
+        grouped_d0 = cast(nc.vector.tensor_copy, raw_d0, "d0")
+        turn(1, 0, 4, turned[1])
+        put_out(0, 0, 4, turned[0], nc.scalar.copy, nc.sync)
+        grouped_d1 = cast(nc.vector.tensor_copy, raw_d1, "d1")
+        multiply(0, 3, x0_blocks, *quantise(grouped_d0, "d0"))
+        multiply(1, 3, x1_blocks, *quantise(grouped_d1, "d1"))
+        squash(2)
+        put_out(1, 0, 4, turned[1], nc.vector.tensor_copy, nc.sync)
+        turn(2, 0, 4, turned[2])
+        squash(3)
+        put_out(2, 0, 4, turned[2], nc.vector.tensor_copy, nc.sync)
+        turn(3, 0, 2, turned[0])
+        turn(3, 2, 2, turned[1])
+        put_out(3, 0, 2, turned[0], nc.vector.tensor_copy, nc.sync)
+        put_out(3, 2, 2, turned[1], nc.scalar.copy, nc.scalar)

@@ -18,6 +18,7 @@ PASSES = 2
 FLOPS = 2 * K * PICKED * DOCS
 BYTES = K * LABELS + K // 32 * LABELS + 4 * K * DOCS + 2 * 4 * LABELS + 2 * PICKED + 4 * DOCS * PICKED
 GAIN_ROW = 126
+SCALE_ROW = 96
 
 
 def tile_picked_zplatt_sig_p_kernel(tc, x_words, x_scales, hT, gain, shift, offs, out):
@@ -30,65 +31,62 @@ def tile_picked_zplatt_sig_p_kernel(tc, x_words, x_scales, hT, gain, shift, offs
             return keep.tile(shape, dtype, name=name, tag=slot or name, align_bytes=64)
 
         offsets = sb([P, PICKED // 16], U16, "offsets")
-        scale_window = sb([P, LABELS], U8, "scale_window")
-        row_window = sb([P, LABELS], F32, "row_window")
+        scale_window = sb([P, LABELS], U8, "scale_window", "slot_scales")
+        row_window = sb([P, LABELS], F32, "row_window", "slot_rows")
+        x_planes = sb([P, PASSES, PICKED], U8, "x_planes")
         h_rows = [hT[512 * o : 512 * (o + 1), :].rearrange("(p j) t -> p j t", j=4) for o in range(PASSES)]
         warm_in = sb([P, 1], F32, "warm_in")
         warm_out = sb([P, 1], F32, "warm_out")
         identity = sb([P, P], F32, "identity")
 
         nc.gpsimd.memset(warm_in[:], 0.0)
-        nc.vector.memset(scale_window[:].bitcast(I32)[:, 0:256], 0)
-        nc.gpsimd.memset(scale_window[:].bitcast(I32)[:, 256:512], 0)
         nc.scalar.activation(warm_out[:], warm_in[:], SIGMOID)
+        nc.gpsimd.memset(scale_window[0:SCALE_ROW, :].bitcast(I32), 0)
         nc.vector.memset(row_window[0:GAIN_ROW, :], 0.0)
+        nc.gpsimd.memset(x_planes[:].rearrange("p o s -> p (o s)").bitcast(I32), 0)
         make_identity(nc, identity[:])
 
-        def load_words(o):
-            window = sb([P, LABELS], I32, "word_window%d" % o)
+        def load_words(o, slot=None):
+            window = sb([P, LABELS], I32, "word_window%d" % o, slot)
             nc.sync.dma_start(window[:], x_words[o].rearrange("p n t -> p (n t)").bitcast(I32))
             return window
 
-        def load_docs(o, t0, width):
-            raw = sb([P, 4, width], F32, "h%d_raw%d" % (o, t0))
-            nc.sync.dma_start(raw[:], h_rows[o][:, :, t0 : t0 + width])
-            return raw
-
         nc.sync.dma_start(offsets[:], offs)
+        nc.sync.dma_start(scale_window[SCALE_ROW:, :].bitcast(I32), x_scales.rearrange("o q n -> q o n").bitcast(I32))
         nc.sync.dma_start(row_window[GAIN_ROW : GAIN_ROW + 1, :], gain[0:1, :])
         nc.sync.dma_start(row_window[GAIN_ROW + 1 : GAIN_ROW + 2, :], shift[0:1, :])
-        window0 = load_words(0)
+        window0 = load_words(0, "slot_x0")
+        h0_raw = sb([P, 4, DOCS], F32, "h0_raw")
+        nc.sync.dma_start(h0_raw[:], h_rows[0])
+
+        x_bytes = sb([P, PICKED], U8, "x_bytes")
+        nc.vector.tensor_copy(x_bytes[:], scale_window[:].indirect(offsets[:]))
         for q in range(4):
             nc.sync.dma_start(
-                scale_window[32 * q : 32 * q + 8, :].bitcast(I32),
-                x_scales[:, 4 * q : 4 * q + 4, :].bitcast(I32),
+                x_planes[32 * q : 32 * q + 4].bitcast(I32),
+                x_bytes[SCALE_ROW + 8 * q : SCALE_ROW + 8 * (q + 1), :].bitcast(I32),
             )
-        raw_ab0 = load_docs(0, 0, 256)
-        window1 = load_words(1)
-        raw_a1 = load_docs(1, 0, P)
-        raw_b1 = load_docs(1, P, P)
-        raw_c0 = load_docs(0, 2 * P, P)
-        raw_c1 = load_docs(1, 2 * P, P)
-        raw_d0 = load_docs(0, 3 * P, P)
-        raw_d1 = load_docs(1, 3 * P, P)
+        h1_first = sb([P, 4, 256], F32, "h1_first", "slot_scales")
+        nc.sync.dma_start(h1_first[:], h_rows[1][:, :, 0:256])
 
         sums = [psum.tile([P, 512], F32, name="sums%d" % b) for b in range(5)]
         turned = [psum.tile([P, 512], F32, name="turned%d" % b) for b in range(3)]
 
         picked_rows = sb([P, PICKED], F32, "picked_rows")
         nc.vector.tensor_copy(picked_rows[:], row_window[:].indirect(offsets[:]))
-        x0_codes = sb([P, PICKED], U32, "x0_codes")
-        nc.vector.tensor_copy(x0_codes[:], window0[:].bitcast(U32).indirect(offsets[:]))
-        x_bytes = sb([P, PICKED], U8, "x_bytes")
-        nc.vector.tensor_copy(x_bytes[:], scale_window[:].indirect(offsets[:]))
+        window1 = load_words(1, "slot_rows")
         for b in range(4):
             nc.tensor.transpose(turned[2][:, P * b : P * (b + 1)], picked_rows[:, P * b : P * (b + 1)], identity[:])
+        platt = sb([P, 4, 2], F32, "platt")
+        nc.scalar.copy(platt[:], turned[2][:].rearrange("p (b r) -> p b r", b=4)[:, :, GAIN_ROW : GAIN_ROW + 2])
 
-        def cast(copy, raw, name):
-            width = raw.shape[2]
-            grouped = sb([P, width, 4], BF16, name + "_grouped")
-            copy(grouped[:].rearrange("p (c i) j -> p c j i", i=4), raw[:].rearrange("p j (c i) -> p c j i", i=4))
-            return grouped
+        def gather_words(window, name, b0, blocks):
+            codes = sb([P, P * blocks], U32, name)
+            nc.vector.tensor_copy(codes[:], window[:].bitcast(U32).indirect(offsets[:, 8 * b0 : 8 * (b0 + blocks)]))
+            return [codes[:, P * b : P * (b + 1)] for b in range(blocks)]
+
+        def cast(copy, grouped, raw):
+            copy(grouped.rearrange("p (c i) j -> p c j i", i=4), raw.rearrange("p j (c i) -> p c j i", i=4))
 
         def quantise(grouped, name):
             width = grouped.shape[1]
@@ -99,10 +97,12 @@ def tile_picked_zplatt_sig_p_kernel(tc, x_words, x_scales, hT, gain, shift, offs
             )
             return codes[:], scales[:]
 
+        chunks = [(0, 256, 0, 2), (256, P, 2, 4), (384, P, 3, 2)]
+
         def region(c, b):
-            if c < 3:
-                return sums[c][:, P * b : P * (b + 1)], b == 0, b == 3
-            return sums[3 + b // 2][:, P * (b % 2) : P * (b % 2 + 1)], b % 2 == 0, b % 2 == 1
+            t0, width, bank, per_bank = chunks[c]
+            i = b % per_bank
+            return sums[bank + b // per_bank][:, i * width : (i + 1) * width], i == 0, i == per_bank - 1
 
         def multiply(o, c, label_codes, codes, scales):
             for b in range(4):
@@ -110,28 +110,31 @@ def tile_picked_zplatt_sig_p_kernel(tc, x_words, x_scales, hT, gain, shift, offs
                 nc.tensor.matmul_mx(
                     out=target,
                     lhsT=label_codes[b].bitcast(FP8X4),
-                    lhsT_scale=x_bytes[4 * o :, P * b : P * (b + 1)],
+                    lhsT_scale=x_planes[:, o, P * b : P * (b + 1)],
                     rhs=codes.bitcast(FP8X4),
                     rhs_scale=scales,
                     start=first and o == 0,
                     stop=last and o == 1,
                 )
 
-        grouped_ab0 = cast(nc.scalar.copy, raw_ab0, "ab0")
-        platt = sb([P, 4, 2], F32, "platt")
-        nc.scalar.copy(platt[:], turned[2][:].rearrange("p (b r) -> p b r", b=4)[:, :, GAIN_ROW : GAIN_ROW + 2])
-        codes_ab0, scales_ab0 = quantise(grouped_ab0, "ab0")
+        x0_blocks = gather_words(window0, "x0_codes", 0, 4)
+        h1_late = sb([P, 4, 256], F32, "h1_late", "slot_x0")
+        nc.sync.dma_start(h1_late[:], h_rows[1][:, :, 256:512])
+        h0_grouped = [sb([P, 256, 4], BF16, "h0_grouped%d" % i) for i in range(2)]
+        cast(nc.scalar.copy, h0_grouped[0][:], h0_raw[:, :, 0:256])
+        cast(nc.vector.tensor_copy, h0_grouped[1][:], h0_raw[:, :, 256:512])
+        codes, scales = quantise(h0_grouped[1], "h0_1")
+        for c in (1, 2):
+            docs = slice(P * (c - 1), P * c)
+            multiply(0, c, x0_blocks, codes[:, docs], scales[:, docs])
+        multiply(0, 0, x0_blocks, *quantise(h0_grouped[0], "h0_0"))
 
-        x0_blocks = [x0_codes[:, P * b : P * (b + 1)] for b in range(4)]
-        for c in range(2):
-            docs = slice(P * c, P * (c + 1))
-            multiply(0, c, x0_blocks, codes_ab0[:, docs], scales_ab0[:, docs])
+        first_grouped = sb([P, 256, 4], BF16, "h1_0_grouped")
+        cast(nc.scalar.copy, first_grouped[:], h1_first[:])
+        h1_first_mx = quantise(first_grouped, "h1_0")
+        x1_blocks = gather_words(window1, "x1_codes0", 0, 2) + gather_words(window1, "x1_codes1", 2, 2)
 
-        x1_codes = sb([P, PICKED], U32, "x1_codes")
-        nc.vector.tensor_copy(x1_codes[:], window1[:].bitcast(U32).indirect(offsets[:]))
-        x1_blocks = [x1_codes[:, P * b : P * (b + 1)] for b in range(4)]
-
-        probs = [sb([P, 4, P], F32, "probs%d" % c) for c in range(4)]
+        probs = [sb([P, 4, chunks[c][1]], F32, "probs%d" % c) for c in range(3)]
 
         def squash(c):
             for b in range(4):
@@ -139,39 +142,34 @@ def tile_picked_zplatt_sig_p_kernel(tc, x_words, x_scales, hT, gain, shift, offs
                     probs[c][:, b, :], region(c, b)[0], SIGMOID, bias=platt[:, b, 1:2], scale=platt[:, b, 0:1]
                 )
 
-        def turn(c, b0, blocks, bank):
-            for i in range(blocks):
-                nc.tensor.transpose(bank[:, P * i : P * (i + 1)], probs[c][:, b0 + i, :], identity[:])
-
         def put_out(c, b0, blocks, bank, copy, queue):
+            t0, width = chunks[c][0:2]
+            groups = width // P
             cols = P * blocks
-            result = sb([P, cols], F32, "result%d_%d" % (c, b0))
-            copy(result[:], bank[:, 0:cols])
-            queue.dma_start(out[P * c : P * (c + 1), P * b0 : P * b0 + cols], result[:])
+            for i in range(blocks):
+                for s in range(groups):
+                    nc.tensor.transpose(
+                        bank[:, cols * s + P * i : cols * s + P * (i + 1)],
+                        probs[c][:, b0 + i, P * s : P * (s + 1)],
+                        identity[:],
+                    )
+            result = sb([P, groups, cols], F32, "result%d_%d" % (c, b0))
+            copy(result[:].rearrange("p s j -> p (s j)"), bank[:, 0 : groups * cols])
+            queue.dma_start(
+                out[t0 : t0 + width, P * b0 : P * b0 + cols].rearrange("(s p) j -> p s j", s=groups), result[:]
+            )
 
-        grouped_a1 = cast(nc.scalar.copy, raw_a1, "a1")
-        grouped_b1 = cast(nc.scalar.copy, raw_b1, "b1")
-        multiply(1, 0, x1_blocks, *quantise(grouped_a1, "a1"))
-        grouped_c0 = cast(nc.vector.tensor_copy, raw_c0, "c0")
-        multiply(1, 1, x1_blocks, *quantise(grouped_b1, "b1"))
+        multiply(1, 0, x1_blocks, *h1_first_mx)
+        late_grouped = [sb([P, P, 4], BF16, "h1_%d_grouped" % c) for c in (1, 2)]
+        for i in range(2):
+            cast(nc.vector.tensor_copy, late_grouped[i][:], h1_late[:, :, P * i : P * (i + 1)])
         squash(0)
-        grouped_c1 = cast(nc.vector.tensor_copy, raw_c1, "c1")
-        multiply(0, 2, x0_blocks, *quantise(grouped_c0, "c0"))
-        turn(0, 0, 4, turned[0])
+        for i in range(2):
+            multiply(1, 1 + i, x1_blocks, *quantise(late_grouped[i], "h1_%d" % (1 + i)))
+        put_out(0, 0, 2, turned[0], nc.vector.tensor_copy, nc.sync)
         squash(1)
-        multiply(1, 2, x1_blocks, *quantise(grouped_c1, "c1"))
-        grouped_d0 = cast(nc.vector.tensor_copy, raw_d0, "d0")
-        turn(1, 0, 4, turned[1])
-        put_out(0, 0, 4, turned[0], nc.scalar.copy, nc.sync)
-        grouped_d1 = cast(nc.vector.tensor_copy, raw_d1, "d1")
-        multiply(0, 3, x0_blocks, *quantise(grouped_d0, "d0"))
-        multiply(1, 3, x1_blocks, *quantise(grouped_d1, "d1"))
+        put_out(0, 2, 2, turned[1], nc.vector.tensor_copy, nc.sync)
         squash(2)
-        put_out(1, 0, 4, turned[1], nc.vector.tensor_copy, nc.sync)
-        turn(2, 0, 4, turned[2])
-        squash(3)
-        put_out(2, 0, 4, turned[2], nc.vector.tensor_copy, nc.sync)
-        turn(3, 0, 2, turned[0])
-        turn(3, 2, 2, turned[1])
-        put_out(3, 0, 2, turned[0], nc.vector.tensor_copy, nc.sync)
-        put_out(3, 2, 2, turned[1], nc.scalar.copy, nc.scalar)
+        put_out(1, 0, 4, turned[2], nc.vector.tensor_copy, nc.sync)
+        put_out(2, 0, 2, turned[0], nc.scalar.copy, nc.scalar)
+        put_out(2, 2, 2, turned[1], nc.vector.tensor_copy, nc.sync)

@@ -77,8 +77,12 @@ def tile_picked_zplatt_sig_p_kernel(tc, x_words, x_scales, hT, gain, shift, offs
         window1 = load_words(1, "slot_rows")
         for b in range(4):
             nc.tensor.transpose(turned[2][:, P * b : P * (b + 1)], picked_rows[:, P * b : P * (b + 1)], identity[:])
+        turned_rows = turned[2][:].rearrange("p (b r) -> p b r", b=4)[:, :, GAIN_ROW : GAIN_ROW + 2]
         platt = sb([P, 4, 2], F32, "platt")
-        nc.scalar.copy(platt[:], turned[2][:].rearrange("p (b r) -> p b r", b=4)[:, :, GAIN_ROW : GAIN_ROW + 2])
+        nc.scalar.copy(platt[:], turned_rows)
+        first_platt = [sb([P, 2, 2], F32, "first_platt%d" % i, "slot_platt%d" % i) for i in range(2)]
+        for i in range(2):
+            nc.scalar.copy(first_platt[i][:], turned_rows[:, 2 * i : 2 * i + 2, :])
 
         def gather_words(window, name, b0, blocks):
             codes = sb([P, P * blocks], U32, name)
@@ -88,10 +92,10 @@ def tile_picked_zplatt_sig_p_kernel(tc, x_words, x_scales, hT, gain, shift, offs
         def cast(copy, grouped, raw):
             copy(grouped.rearrange("p (c i) j -> p c j i", i=4), raw.rearrange("p j (c i) -> p c j i", i=4))
 
-        def quantise(grouped, name):
+        def quantise(grouped, name, slot=None):
             width = grouped.shape[1]
             codes = sb([P, width], U32, name + "_codes")
-            scales = sb([P, width], U8, name + "_scales")
+            scales = sb([P, width], U8, name + "_scales", slot)
             nc.vector.quantize_mx(
                 out=codes[:].bitcast(FP8X4), scales=scales[:], in_=grouped[:].rearrange("p t j -> p (t j)")
             )
@@ -138,9 +142,8 @@ def tile_picked_zplatt_sig_p_kernel(tc, x_words, x_scales, hT, gain, shift, offs
 
         def squash(c):
             for b in range(4):
-                nc.scalar.activation(
-                    probs[c][:, b, :], region(c, b)[0], SIGMOID, bias=platt[:, b, 1:2], scale=platt[:, b, 0:1]
-                )
+                pair = first_platt[b // 2][:, b % 2, :] if c == 0 else platt[:, b, :]
+                nc.scalar.activation(probs[c][:, b, :], region(c, b)[0], SIGMOID, bias=pair[:, 1:2], scale=pair[:, 0:1])
 
         def put_out(c, b0, blocks, bank, copy, queue):
             t0, width = chunks[c][0:2]
@@ -160,16 +163,16 @@ def tile_picked_zplatt_sig_p_kernel(tc, x_words, x_scales, hT, gain, shift, offs
             )
 
         multiply(1, 0, x1_blocks, *h1_first_mx)
-        late_grouped = [sb([P, P, 4], BF16, "h1_%d_grouped" % c) for c in (1, 2)]
-        for i in range(2):
-            cast(nc.vector.tensor_copy, late_grouped[i][:], h1_late[:, :, P * i : P * (i + 1)])
         squash(0)
         for i in range(2):
-            multiply(1, 1 + i, x1_blocks, *quantise(late_grouped[i], "h1_%d" % (1 + i)))
+            grouped = sb([P, P, 4], BF16, "h1_%d_grouped" % (1 + i), "slot_late")
+            cast(nc.vector.tensor_copy, grouped[:], h1_late[:, :, P * i : P * (i + 1)])
+            multiply(1, 1 + i, x1_blocks, *quantise(grouped, "h1_%d" % (1 + i), "slot_platt%d" % i))
         put_out(0, 0, 2, turned[0], nc.vector.tensor_copy, nc.sync)
         squash(1)
         put_out(0, 2, 2, turned[1], nc.vector.tensor_copy, nc.sync)
         squash(2)
         put_out(1, 0, 4, turned[2], nc.vector.tensor_copy, nc.sync)
-        put_out(2, 0, 2, turned[0], nc.scalar.copy, nc.scalar)
-        put_out(2, 2, 2, turned[1], nc.vector.tensor_copy, nc.sync)
+        put_out(2, 0, 2, sums[0], nc.scalar.copy, nc.sync)
+        put_out(2, 2, 1, sums[1], nc.vector.tensor_copy, nc.sync)
+        put_out(2, 3, 1, sums[2], nc.scalar.copy, nc.scalar)

@@ -17,8 +17,7 @@ K, LABELS, PICKED, DOCS = 1024, 2048, 512, 512
 PASSES = 2
 FLOPS = 2 * K * PICKED * DOCS
 BYTES = K * LABELS + K // 32 * LABELS + 4 * K * DOCS + 2 * 4 * LABELS + 2 * PICKED + 4 * DOCS * PICKED
-GAIN_ROW = 126
-SCALE_ROW = 96
+GAIN_ROW, SHIFT_ROW = 63, 127
 
 
 def tile_picked_zplatt_sig_p_kernel(tc, x_words, x_scales, hT, gain, shift, offs, out):
@@ -41,8 +40,10 @@ def tile_picked_zplatt_sig_p_kernel(tc, x_words, x_scales, hT, gain, shift, offs
 
         nc.gpsimd.memset(warm_in[:], 0.0)
         nc.scalar.activation(warm_out[:], warm_in[:], SIGMOID)
-        nc.gpsimd.memset(scale_window[0:SCALE_ROW, :].bitcast(I32), 0)
-        nc.vector.memset(row_window[0:GAIN_ROW, :], 0.0)
+        nc.gpsimd.memset(scale_window[32:64, :].bitcast(I32), 0)
+        nc.vector.memset(scale_window[64:P, :].bitcast(I32), 0)
+        nc.vector.memset(row_window[GAIN_ROW + 1 : SHIFT_ROW, :], 0.0)
+        nc.gpsimd.memset(row_window[0:GAIN_ROW, :], 0.0)
         nc.gpsimd.memset(x_planes[:].rearrange("p o s -> p (o s)").bitcast(I32), 0)
         make_identity(nc, identity[:])
 
@@ -52,9 +53,9 @@ def tile_picked_zplatt_sig_p_kernel(tc, x_words, x_scales, hT, gain, shift, offs
             return window
 
         nc.sync.dma_start(offsets[:], offs)
-        nc.sync.dma_start(scale_window[SCALE_ROW:, :].bitcast(I32), x_scales.rearrange("o q n -> q o n").bitcast(I32))
+        nc.sync.dma_start(scale_window[0:32, :].bitcast(I32), x_scales.rearrange("o q n -> q o n").bitcast(I32))
         nc.sync.dma_start(row_window[GAIN_ROW : GAIN_ROW + 1, :], gain[0:1, :])
-        nc.sync.dma_start(row_window[GAIN_ROW + 1 : GAIN_ROW + 2, :], shift[0:1, :])
+        nc.sync.dma_start(row_window[SHIFT_ROW : SHIFT_ROW + 1, :], shift[0:1, :])
         window0 = load_words(0, "slot_x0")
         h0_raw = sb([P, 4, DOCS], F32, "h0_raw")
         nc.sync.dma_start(h0_raw[:], h_rows[0])
@@ -64,25 +65,22 @@ def tile_picked_zplatt_sig_p_kernel(tc, x_words, x_scales, hT, gain, shift, offs
         for q in range(4):
             nc.sync.dma_start(
                 x_planes[32 * q : 32 * q + 4].bitcast(I32),
-                x_bytes[SCALE_ROW + 8 * q : SCALE_ROW + 8 * (q + 1), :].bitcast(I32),
+                x_bytes[8 * q : 8 * (q + 1), :].bitcast(I32),
             )
-        h1_first = sb([P, 4, 256], F32, "h1_first", "slot_scales")
-        nc.sync.dma_start(h1_first[:], h_rows[1][:, :, 0:256])
+        window1 = load_words(1, "slot_scales")
 
-        sums = [psum.tile([P, 512], F32, name="sums%d" % b) for b in range(5)]
-        turned = [psum.tile([P, 512], F32, name="turned%d" % b) for b in range(3)]
+        sums = [psum.tile([P, 512], F32, name="sums%d" % b) for b in range(7)]
+        spare = psum.tile([P, 512], F32, name="spare")
 
         picked_rows = sb([P, PICKED], F32, "picked_rows")
         nc.vector.tensor_copy(picked_rows[:], row_window[:].indirect(offsets[:]))
-        window1 = load_words(1, "slot_rows")
+        h1_first = sb([P, 4, 256], F32, "h1_first", "slot_rows")
+        nc.sync.dma_start(h1_first[:], h_rows[1][:, :, 0:256])
         for b in range(4):
-            nc.tensor.transpose(turned[2][:, P * b : P * (b + 1)], picked_rows[:, P * b : P * (b + 1)], identity[:])
-        turned_rows = turned[2][:].rearrange("p (b r) -> p b r", b=4)[:, :, GAIN_ROW : GAIN_ROW + 2]
+            nc.tensor.transpose(spare[:, P * b : P * (b + 1)], picked_rows[:, P * b : P * (b + 1)], identity[:])
+        turned_rows = spare[:].rearrange("p (b r) -> p b r", b=4)[:, :, GAIN_ROW :: SHIFT_ROW - GAIN_ROW]
         platt = sb([P, 4, 2], F32, "platt")
         nc.scalar.copy(platt[:], turned_rows)
-        first_platt = [sb([P, 2, 2], F32, "first_platt%d" % i, "slot_platt%d" % i) for i in range(2)]
-        for i in range(2):
-            nc.scalar.copy(first_platt[i][:], turned_rows[:, 2 * i : 2 * i + 2, :])
 
         def gather_words(window, name, b0, blocks):
             codes = sb([P, P * blocks], U32, name)
@@ -92,16 +90,16 @@ def tile_picked_zplatt_sig_p_kernel(tc, x_words, x_scales, hT, gain, shift, offs
         def cast(copy, grouped, raw):
             copy(grouped.rearrange("p (c i) j -> p c j i", i=4), raw.rearrange("p j (c i) -> p c j i", i=4))
 
-        def quantise(grouped, name, slot=None):
+        def quantise(grouped, name):
             width = grouped.shape[1]
             codes = sb([P, width], U32, name + "_codes")
-            scales = sb([P, width], U8, name + "_scales", slot)
+            scales = sb([P, width], U8, name + "_scales")
             nc.vector.quantize_mx(
                 out=codes[:].bitcast(FP8X4), scales=scales[:], in_=grouped[:].rearrange("p t j -> p (t j)")
             )
             return codes[:], scales[:]
 
-        chunks = [(0, 256, 0, 2), (256, P, 2, 4), (384, P, 3, 2)]
+        chunks = [(0, 256, 0, 1), (256, P, 4, 4), (384, P, 5, 2)]
 
         def region(c, b):
             t0, width, bank, per_bank = chunks[c]
@@ -133,46 +131,43 @@ def tile_picked_zplatt_sig_p_kernel(tc, x_words, x_scales, hT, gain, shift, offs
             multiply(0, c, x0_blocks, codes[:, docs], scales[:, docs])
         multiply(0, 0, x0_blocks, *quantise(h0_grouped[0], "h0_0"))
 
+        x1_blocks = gather_words(window1, "x1_codes", 0, 4)
         first_grouped = sb([P, 256, 4], BF16, "h1_0_grouped")
-        cast(nc.scalar.copy, first_grouped[:], h1_first[:])
+        cast(nc.scalar.copy, first_grouped[:, P:256, :], h1_first[:, :, P:256])
+        cast(nc.vector.tensor_copy, first_grouped[:, 0:P, :], h1_first[:, :, 0:P])
         h1_first_mx = quantise(first_grouped, "h1_0")
-        x1_blocks = gather_words(window1, "x1_codes0", 0, 2) + gather_words(window1, "x1_codes1", 2, 2)
 
         probs = [sb([P, 4, chunks[c][1]], F32, "probs%d" % c) for c in range(3)]
 
         def squash(c):
             for b in range(4):
-                pair = first_platt[b // 2][:, b % 2, :] if c == 0 else platt[:, b, :]
-                nc.scalar.activation(probs[c][:, b, :], region(c, b)[0], SIGMOID, bias=pair[:, 1:2], scale=pair[:, 0:1])
+                nc.scalar.activation(
+                    probs[c][:, b, :], region(c, b)[0], SIGMOID, bias=platt[:, b, 1:2], scale=platt[:, b, 0:1]
+                )
 
-        def put_out(c, b0, blocks, bank, copy, queue):
-            t0, width = chunks[c][0:2]
-            groups = width // P
-            cols = P * blocks
-            for i in range(blocks):
-                for s in range(groups):
-                    nc.tensor.transpose(
-                        bank[:, cols * s + P * i : cols * s + P * (i + 1)],
-                        probs[c][:, b0 + i, P * s : P * (s + 1)],
-                        identity[:],
-                    )
-            result = sb([P, groups, cols], F32, "result%d_%d" % (c, b0))
-            copy(result[:].rearrange("p s j -> p (s j)"), bank[:, 0 : groups * cols])
-            queue.dma_start(
-                out[t0 : t0 + width, P * b0 : P * b0 + cols].rearrange("(s p) j -> p s j", s=groups), result[:]
-            )
+        def put_out(c, s, b0, bank, copy, queue):
+            t0 = chunks[c][0] + P * s
+            for i in range(2):
+                nc.tensor.transpose(bank[:, P * i : P * (i + 1)], probs[c][:, b0 + i, P * s : P * (s + 1)], identity[:])
+            result = sb([P, 2 * P], F32, "result%d_%d" % (t0, b0))
+            copy(result[:], bank[:, 0 : 2 * P])
+            queue.dma_start(out[t0 : t0 + P, P * b0 : P * (b0 + 2)], result[:])
 
         multiply(1, 0, x1_blocks, *h1_first_mx)
         squash(0)
+        late_grouped = [sb([P, P, 4], BF16, "h1_1_grouped"), sb([P, P, 4], BF16, "h1_2_grouped")]
         for i in range(2):
-            grouped = sb([P, P, 4], BF16, "h1_%d_grouped" % (1 + i), "slot_late")
-            cast(nc.vector.tensor_copy, grouped[:], h1_late[:, :, P * i : P * (i + 1)])
-            multiply(1, 1 + i, x1_blocks, *quantise(grouped, "h1_%d" % (1 + i), "slot_platt%d" % i))
-        put_out(0, 0, 2, turned[0], nc.vector.tensor_copy, nc.sync)
+            cast(nc.vector.tensor_copy, late_grouped[i][:], h1_late[:, :, P * i : P * (i + 1)])
+        late_mx = [quantise(late_grouped[i], "h1_%d" % (1 + i)) for i in range(2)]
+        multiply(1, 1, x1_blocks, *late_mx[0])
+        multiply(1, 2, x1_blocks, *late_mx[1])
+        put_out(0, 0, 0, spare, nc.vector.tensor_copy, nc.sync)
+        put_out(0, 1, 0, sums[0], nc.vector.tensor_copy, nc.sync)
         squash(1)
-        put_out(0, 2, 2, turned[1], nc.vector.tensor_copy, nc.sync)
+        put_out(0, 0, 2, sums[1], nc.vector.tensor_copy, nc.sync)
+        put_out(0, 1, 2, sums[2], nc.vector.tensor_copy, nc.sync)
         squash(2)
-        put_out(1, 0, 4, turned[2], nc.vector.tensor_copy, nc.sync)
-        put_out(2, 0, 2, sums[0], nc.scalar.copy, nc.sync)
-        put_out(2, 2, 1, sums[1], nc.vector.tensor_copy, nc.sync)
-        put_out(2, 3, 1, sums[2], nc.scalar.copy, nc.scalar)
+        put_out(1, 0, 0, sums[3], nc.vector.tensor_copy, nc.sync)
+        put_out(1, 0, 2, spare, nc.scalar.copy, nc.sync)
+        put_out(2, 0, 0, sums[4], nc.vector.tensor_copy, nc.sync)
+        put_out(2, 0, 2, sums[0], nc.scalar.copy, nc.scalar)

@@ -17,7 +17,8 @@ K, LABELS, PICKED, DOCS = 1024, 2048, 512, 512
 PASSES = 2
 FLOPS = 2 * K * PICKED * DOCS
 BYTES = K * LABELS + K // 32 * LABELS + 4 * K * DOCS + 2 * 4 * LABELS + 2 * PICKED + 4 * DOCS * PICKED
-GAIN_ROW, SHIFT_ROW = 63, 127
+GAIN_ROW = 126
+SCALE_ROW = 96
 
 
 def tile_picked_zplatt_sig_p_kernel(tc, x_words, x_scales, hT, gain, shift, offs, out):
@@ -40,10 +41,8 @@ def tile_picked_zplatt_sig_p_kernel(tc, x_words, x_scales, hT, gain, shift, offs
 
         nc.gpsimd.memset(warm_in[:], 0.0)
         nc.scalar.activation(warm_out[:], warm_in[:], SIGMOID)
-        nc.gpsimd.memset(scale_window[32:64, :].bitcast(I32), 0)
-        nc.vector.memset(scale_window[64:P, :].bitcast(I32), 0)
-        nc.vector.memset(row_window[GAIN_ROW + 1 : SHIFT_ROW, :], 0.0)
-        nc.gpsimd.memset(row_window[0:GAIN_ROW, :], 0.0)
+        nc.gpsimd.memset(scale_window[0:SCALE_ROW, :].bitcast(I32), 0)
+        nc.vector.memset(row_window[0:GAIN_ROW, :], 0.0)
         nc.gpsimd.memset(x_planes[:].rearrange("p o s -> p (o s)").bitcast(I32), 0)
         make_identity(nc, identity[:])
 
@@ -53,9 +52,9 @@ def tile_picked_zplatt_sig_p_kernel(tc, x_words, x_scales, hT, gain, shift, offs
             return window
 
         nc.sync.dma_start(offsets[:], offs)
-        nc.sync.dma_start(scale_window[0:32, :].bitcast(I32), x_scales.rearrange("o q n -> q o n").bitcast(I32))
+        nc.sync.dma_start(scale_window[SCALE_ROW:, :].bitcast(I32), x_scales.rearrange("o q n -> q o n").bitcast(I32))
         nc.sync.dma_start(row_window[GAIN_ROW : GAIN_ROW + 1, :], gain[0:1, :])
-        nc.sync.dma_start(row_window[SHIFT_ROW : SHIFT_ROW + 1, :], shift[0:1, :])
+        nc.sync.dma_start(row_window[GAIN_ROW + 1 : GAIN_ROW + 2, :], shift[0:1, :])
         window0 = load_words(0, "slot_x0")
         h0_raw = sb([P, 4, DOCS], F32, "h0_raw")
         nc.sync.dma_start(h0_raw[:], h_rows[0])
@@ -65,7 +64,7 @@ def tile_picked_zplatt_sig_p_kernel(tc, x_words, x_scales, hT, gain, shift, offs
         for q in range(4):
             nc.sync.dma_start(
                 x_planes[32 * q : 32 * q + 4].bitcast(I32),
-                x_bytes[8 * q : 8 * (q + 1), :].bitcast(I32),
+                x_bytes[SCALE_ROW + 8 * q : SCALE_ROW + 8 * (q + 1), :].bitcast(I32),
             )
         window1 = load_words(1, "slot_scales")
 
@@ -78,7 +77,7 @@ def tile_picked_zplatt_sig_p_kernel(tc, x_words, x_scales, hT, gain, shift, offs
         nc.sync.dma_start(h1_first[:], h_rows[1][:, :, 0:256])
         for b in range(4):
             nc.tensor.transpose(spare[:, P * b : P * (b + 1)], picked_rows[:, P * b : P * (b + 1)], identity[:])
-        turned_rows = spare[:].rearrange("p (b r) -> p b r", b=4)[:, :, GAIN_ROW :: SHIFT_ROW - GAIN_ROW]
+        turned_rows = spare[:].rearrange("p (b r) -> p b r", b=4)[:, :, GAIN_ROW : GAIN_ROW + 2]
         platt = sb([P, 4, 2], F32, "platt")
         nc.scalar.copy(platt[:], turned_rows)
 

@@ -11,6 +11,8 @@ U16 = mybir.dt.uint16
 U8 = mybir.dt.uint8
 FP8X4 = mybir.dt.float8_e4m3fn_x4
 SIGMOID = mybir.ActivationFunctionType.Sigmoid
+MULT = mybir.AluOpType.mult
+ADD = mybir.AluOpType.add
 
 P = 128
 K, LABELS, PICKED, DOCS = 1024, 2048, 512, 512
@@ -18,21 +20,26 @@ PASSES = 2
 FLOPS = 2 * K * PICKED * DOCS
 BYTES = K * LABELS + K // 32 * LABELS + 4 * K * DOCS + 2 * 4 * LABELS + 2 * PICKED + 4 * DOCS * PICKED
 GAIN_ROW = 126
-SCALE_ROW = 96
+SCALE_ROWS = 32
+HALF = 256
+KIB = 1024
 
 
 def tile_picked_zplatt_sig_p_kernel(tc, x_words, x_scales, hT, gain, shift, offs, out):
     nc = tc.nc
     with ExitStack() as ctx:
         keep = ctx.enter_context(tc.tile_pool(name="keep", bufs=1))
+        reused = ctx.enter_context(tc.tile_pool(name="reused", bufs=1))
         psum = ctx.enter_context(tc.psum_pool(name="psum", bufs=1))
 
-        def sb(shape, dtype, name, slot=None):
-            return keep.tile(shape, dtype, name=name, tag=slot or name, align_bytes=64)
+        def sb(shape, dtype, name, at=None):
+            if at is None:
+                return keep.tile(shape, dtype, name=name, align_bytes=64)
+            return reused.tile(shape, dtype, name=name, align_bytes=64, offset=at)
 
         offsets = sb([P, PICKED // 16], U16, "offsets")
-        scale_window = sb([P, LABELS], U8, "scale_window", "slot_scales")
-        row_window = sb([P, LABELS], F32, "row_window", "slot_rows")
+        scale_window = sb([P, LABELS], U8, "scale_window", 47 * KIB)
+        row_window = sb([P, LABELS], F32, "row_window", 6 * KIB)
         x_planes = sb([P, PASSES, PICKED], U8, "x_planes")
         h_rows = [hT[512 * o : 512 * (o + 1), :].rearrange("(p j) t -> p j t", j=4) for o in range(PASSES)]
         warm_in = sb([P, 1], F32, "warm_in")
@@ -40,133 +47,174 @@ def tile_picked_zplatt_sig_p_kernel(tc, x_words, x_scales, hT, gain, shift, offs
         identity = sb([P, P], F32, "identity")
 
         nc.gpsimd.memset(warm_in[:], 0.0)
+        nc.gpsimd.memset(scale_window[64:P, :].bitcast(I32), 0)
         nc.scalar.activation(warm_out[:], warm_in[:], SIGMOID)
-        nc.gpsimd.memset(scale_window[0:SCALE_ROW, :].bitcast(I32), 0)
+        nc.vector.memset(scale_window[32:64, :].bitcast(I32), 0)
         nc.vector.memset(row_window[0:GAIN_ROW, :], 0.0)
-        nc.gpsimd.memset(x_planes[:].rearrange("p o s -> p (o s)").bitcast(I32), 0)
         make_identity(nc, identity[:])
+        nc.gpsimd.memset(x_planes[:].rearrange("p o s -> p (o s)").bitcast(I32), 0)
 
-        def load_words(o, slot=None):
-            window = sb([P, LABELS], I32, "word_window%d" % o, slot)
+        def load_words(o, at=None):
+            window = sb([P, LABELS], I32, "word_window%d" % o, at)
             nc.sync.dma_start(window[:], x_words[o].rearrange("p n t -> p (n t)").bitcast(I32))
             return window
 
+        def load_docs(o, first, width, at=None):
+            raw = sb([P, 4, width], F32, "h%d_%d_raw" % (o, first), at)
+            nc.sync.dma_start(raw[:], h_rows[o][:, :, first : first + width])
+            return raw
+
         nc.sync.dma_start(offsets[:], offs)
-        nc.sync.dma_start(scale_window[SCALE_ROW:, :].bitcast(I32), x_scales.rearrange("o q n -> q o n").bitcast(I32))
+        nc.sync.dma_start(scale_window[0:SCALE_ROWS, :].bitcast(I32), x_scales.rearrange("o q n -> q o n").bitcast(I32))
         nc.sync.dma_start(row_window[GAIN_ROW : GAIN_ROW + 1, :], gain[0:1, :])
         nc.sync.dma_start(row_window[GAIN_ROW + 1 : GAIN_ROW + 2, :], shift[0:1, :])
-        window0 = load_words(0, "slot_x0")
-        h0_raw = sb([P, 4, DOCS], F32, "h0_raw")
-        nc.sync.dma_start(h0_raw[:], h_rows[0])
+        window0 = load_words(0, 18 * KIB)
+        h0a_raw = load_docs(0, 0, HALF, 36 * KIB)
+        h1a_raw = load_docs(1, 0, HALF)
 
         x_bytes = sb([P, PICKED], U8, "x_bytes")
         nc.vector.tensor_copy(x_bytes[:], scale_window[:].indirect(offsets[:]))
         for q in range(4):
             nc.sync.dma_start(
                 x_planes[32 * q : 32 * q + 4].bitcast(I32),
-                x_bytes[SCALE_ROW + 8 * q : SCALE_ROW + 8 * (q + 1), :].bitcast(I32),
+                x_bytes[8 * q : 8 * (q + 1), :].bitcast(I32),
             )
-        window1 = load_words(1, "slot_scales")
+        window1 = load_words(1, 40 * KIB)
 
-        sums = [psum.tile([P, 512], F32, name="sums%d" % b) for b in range(7)]
-        spare = psum.tile([P, 512], F32, name="spare")
+        banks = [psum.tile([P, 512], F32, name="bank%d" % b) for b in range(8)]
 
-        picked_rows = sb([P, PICKED], F32, "picked_rows")
-        nc.vector.tensor_copy(picked_rows[:], row_window[:].indirect(offsets[:]))
-        h1_first = sb([P, 4, 256], F32, "h1_first", "slot_rows")
-        nc.sync.dma_start(h1_first[:], h_rows[1][:, :, 0:256])
-        for b in range(4):
-            nc.tensor.transpose(spare[:, P * b : P * (b + 1)], picked_rows[:, P * b : P * (b + 1)], identity[:])
-        turned_rows = spare[:].rearrange("p (b r) -> p b r", b=4)[:, :, GAIN_ROW : GAIN_ROW + 2]
-        platt = sb([P, 4, 2], F32, "platt")
-        nc.scalar.copy(platt[:], turned_rows)
-
-        def gather_words(window, name, b0, blocks):
-            codes = sb([P, P * blocks], U32, name)
-            nc.vector.tensor_copy(codes[:], window[:].bitcast(U32).indirect(offsets[:, 8 * b0 : 8 * (b0 + blocks)]))
-            return [codes[:, P * b : P * (b + 1)] for b in range(blocks)]
+        def gather_words(window, name, at):
+            codes = sb([P, PICKED], U32, name, at)
+            nc.vector.tensor_copy(codes[:], window[:].bitcast(U32).indirect(offsets[:]))
+            return codes
 
         def cast(copy, grouped, raw):
             copy(grouped.rearrange("p (c i) j -> p c j i", i=4), raw.rearrange("p j (c i) -> p c j i", i=4))
 
-        def quantise(grouped, name):
+        def quantise(grouped, name, at=None):
             width = grouped.shape[1]
             codes = sb([P, width], U32, name + "_codes")
-            scales = sb([P, width], U8, name + "_scales")
+            scales = sb([P, width], U8, name + "_scales", at)
             nc.vector.quantize_mx(
                 out=codes[:].bitcast(FP8X4), scales=scales[:], in_=grouped[:].rearrange("p t j -> p (t j)")
             )
             return codes[:], scales[:]
 
-        chunks = [(0, 256, 0, 1), (256, P, 4, 4), (384, P, 5, 2)]
+        def sums(chunk, b):
+            held, width, per_bank = chunk
+            return banks[held[b // per_bank]][:, width * (b % per_bank) : width * (b % per_bank + 1)]
 
-        def region(c, b):
-            t0, width, bank, per_bank = chunks[c]
-            i = b % per_bank
-            return sums[bank + b // per_bank][:, i * width : (i + 1) * width], i == 0, i == per_bank - 1
-
-        def multiply(o, c, label_codes, codes, scales):
+        def multiply(o, chunk, label_codes, codes, scales):
+            per_bank = chunk[2]
             for b in range(4):
-                target, first, last = region(c, b)
                 nc.tensor.matmul_mx(
-                    out=target,
-                    lhsT=label_codes[b].bitcast(FP8X4),
+                    out=sums(chunk, b),
+                    lhsT=label_codes[:, P * b : P * (b + 1)].bitcast(FP8X4),
                     lhsT_scale=x_planes[:, o, P * b : P * (b + 1)],
                     rhs=codes.bitcast(FP8X4),
                     rhs_scale=scales,
-                    start=first and o == 0,
-                    stop=last and o == 1,
+                    start=b % per_bank == 0 and o == 0,
+                    stop=b % per_bank == per_bank - 1 and o == 1,
                 )
 
-        x0_blocks = gather_words(window0, "x0_codes", 0, 4)
-        h1_late = sb([P, 4, 256], F32, "h1_late", "slot_x0")
-        nc.sync.dma_start(h1_late[:], h_rows[1][:, :, 256:512])
-        h0_grouped = [sb([P, 256, 4], BF16, "h0_grouped%d" % i) for i in range(2)]
-        cast(nc.scalar.copy, h0_grouped[0][:], h0_raw[:, :, 0:256])
-        cast(nc.vector.tensor_copy, h0_grouped[1][:], h0_raw[:, :, 256:512])
-        codes, scales = quantise(h0_grouped[1], "h0_1")
-        for c in (1, 2):
-            docs = slice(P * (c - 1), P * c)
-            multiply(0, c, x0_blocks, codes[:, docs], scales[:, docs])
-        multiply(0, 0, x0_blocks, *quantise(h0_grouped[0], "h0_0"))
+        early, third, fourth = ((0, 1, 2, 3), HALF, 1), ((3, 2), P, 2), ((4, 5), P, 2)
+        picked_rows = sb([P, PICKED], F32, "picked_rows", 48 * KIB)
+        nc.vector.tensor_copy(picked_rows[:], row_window[:].indirect(offsets[:]))
+        h0b_raw = load_docs(0, HALF, HALF, 10 * KIB)
+        for b in range(4):
+            nc.tensor.transpose(banks[7][:, P * b : P * (b + 1)], picked_rows[:, P * b : P * (b + 1)], identity[:])
+        turned_rows = banks[7][:].rearrange("p (b r) -> p b r", b=4)[:, :, GAIN_ROW : GAIN_ROW + 2]
 
-        x1_blocks = gather_words(window1, "x1_codes", 0, 4)
-        first_grouped = sb([P, 256, 4], BF16, "h1_0_grouped")
-        cast(nc.scalar.copy, first_grouped[:, P:256, :], h1_first[:, :, P:256])
-        cast(nc.vector.tensor_copy, first_grouped[:, 0:P, :], h1_first[:, :, 0:P])
-        h1_first_mx = quantise(first_grouped, "h1_0")
+        x0_blocks = gather_words(window0, "x0_codes", 6 * KIB)
+        late_raw = load_docs(1, HALF, HALF, 22 * KIB)
+        for b in range(2):
+            nc.tensor.matmul_mx(
+                out=banks[4][:],
+                lhsT=x0_blocks[:, 0:P].bitcast(FP8X4),
+                lhsT_scale=x_planes[:, 0, 0:P],
+                rhs=x0_blocks[:].bitcast(FP8X4),
+                rhs_scale=x_planes[:, 0, :],
+                start=True,
+                stop=True,
+            )
+        h0a_grouped = sb([P, HALF, 4], BF16, "h0a_grouped")
+        cast(nc.scalar.copy, h0a_grouped[:], h0a_raw[:])
+        platt = sb([P, 4, 2], F32, "platt", 36 * KIB)
+        nc.scalar.copy(platt[:], turned_rows)
+        h1a_grouped = sb([P, HALF, 4], BF16, "h1a_grouped", 18 * KIB)
+        cast(nc.vector.tensor_copy, h1a_grouped[:], h1a_raw[:])
+        multiply(0, early, x0_blocks, *quantise(h0a_grouped, "h0a"))
+        h1a_mx = quantise(h1a_grouped, "h1a")
 
-        probs = [sb([P, 4, chunks[c][1]], F32, "probs%d" % c) for c in range(3)]
+        x1_blocks = sb([P, PICKED], U32, "x1_codes", 18 * KIB)
+        for side in range(2):
+            nc.vector.tensor_copy(
+                x1_blocks[:, HALF * side : HALF * (side + 1)],
+                window1[:].bitcast(U32).indirect(offsets[:, 16 * side : 16 * (side + 1)]),
+            )
+        multiply(1, early, x1_blocks, *h1a_mx)
 
-        def squash(c):
-            for b in range(4):
-                nc.scalar.activation(
-                    probs[c][:, b, :], region(c, b)[0], SIGMOID, bias=platt[:, b, 1:2], scale=platt[:, b, 0:1]
-                )
+        def squash(target, source, b):
+            nc.scalar.activation(target, source, SIGMOID, bias=platt[:, b, 1:2], scale=platt[:, b, 0:1])
 
-        def put_out(c, s, b0, bank, copy, queue):
-            t0 = chunks[c][0] + P * s
+        def affine(target, source, b):
+            nc.vector.tensor_scalar(target, source, platt[:, b, 0:1], platt[:, b, 1:2], MULT, ADD)
+
+        probs_a = sb([P, 4, HALF], F32, "probs_a")
+        for b in range(4):
+            squash(probs_a[:, b, :], sums(early, b), b)
+
+        h0b_grouped = sb([P, HALF, 4], BF16, "h0b_grouped", 40 * KIB)
+        cast(nc.vector.tensor_copy, h0b_grouped[:], h0b_raw[:])
+        codes, scales = quantise(h0b_grouped, "h0b")
+        late_grouped = [sb([P, P, 4], BF16, "late_grouped%d" % s, (40 + s) * KIB) for s in range(2)]
+        for s in range(2):
+            cast(nc.vector.tensor_copy, late_grouped[s][:], late_raw[:, :, P * s : P * (s + 1)])
+        late_mx = [quantise(late_grouped[s], "late%d" % s) for s in range(2)]
+
+        def turn(target, sources):
             for i in range(2):
-                nc.tensor.transpose(bank[:, P * i : P * (i + 1)], probs[c][:, b0 + i, P * s : P * (s + 1)], identity[:])
-            result = sb([P, 2 * P], F32, "result%d_%d" % (t0, b0))
-            copy(result[:], bank[:, 0 : 2 * P])
-            queue.dma_start(out[t0 : t0 + P, P * b0 : P * (b0 + 2)], result[:])
+                nc.tensor.transpose(target[:, P * i : P * (i + 1)], sources[i], identity[:])
+            return target[:, 0:HALF]
 
-        multiply(1, 0, x1_blocks, *h1_first_mx)
-        squash(0)
-        late_grouped = [sb([P, P, 4], BF16, "h1_1_grouped"), sb([P, P, 4], BF16, "h1_2_grouped")]
-        for i in range(2):
-            cast(nc.vector.tensor_copy, late_grouped[i][:], h1_late[:, :, P * i : P * (i + 1)])
-        late_mx = [quantise(late_grouped[i], "h1_%d" % (1 + i)) for i in range(2)]
-        multiply(1, 1, x1_blocks, *late_mx[0])
-        multiply(1, 2, x1_blocks, *late_mx[1])
-        put_out(0, 0, 0, spare, nc.vector.tensor_copy, nc.sync)
-        put_out(0, 1, 0, sums[0], nc.vector.tensor_copy, nc.sync)
-        squash(1)
-        put_out(0, 0, 2, sums[1], nc.vector.tensor_copy, nc.sync)
-        put_out(0, 1, 2, sums[2], nc.vector.tensor_copy, nc.sync)
-        squash(2)
-        put_out(1, 0, 0, sums[3], nc.vector.tensor_copy, nc.sync)
-        put_out(1, 0, 2, spare, nc.scalar.copy, nc.sync)
-        put_out(2, 0, 0, sums[4], nc.vector.tensor_copy, nc.sync)
-        put_out(2, 0, 2, sums[0], nc.scalar.copy, nc.scalar)
+        def early_pair(side, s):
+            return [probs_a[:, 2 * side + i, P * s : P * (s + 1)] for i in range(2)]
+
+        early_rows = out[0:HALF, :].rearrange("(s p) l -> p s l", s=2)
+        early_left = sb([P, 2, HALF], F32, "early_left")
+        for s in range(2):
+            nc.scalar.copy(early_left[:, s, :], turn(banks[4 + s], early_pair(0, s)))
+        nc.sync.dma_start(early_rows[:, :, 0:HALF], early_left[:])
+        early_right = sb([P, 2, HALF], F32, "early_right")
+        for s in range(2):
+            turn(banks[6][:, HALF * s : HALF * (s + 1)], early_pair(1, s))
+        nc.scalar.copy(early_right[:], banks[6][:].rearrange("p (s l) -> p s l", s=2))
+        nc.sync.dma_start(early_rows[:, :, HALF:PICKED], early_right[:])
+
+        def first_step(chunk, name):
+            left = sb([P, 2, P], F32, name + "_left")
+            right = sb([P, 2, P], F32, name + "_right")
+            for i in range(2):
+                squash(left[:, i, :], sums(chunk, i), i)
+                affine(right[:, i, :], sums(chunk, 2 + i), 2 + i)
+            return left, right
+
+        def second_step(left, right, left_bank, right_bank, name):
+            result = sb([P, PICKED], F32, name)
+            turned_left = turn(left_bank, [left[:, i, :] for i in range(2)])
+            turned_right = turn(right_bank, [right[:, i, :] for i in range(2)])
+            nc.vector.tensor_copy(result[:, 0:HALF], turned_left)
+            nc.scalar.activation(result[:, HALF:PICKED], turned_right, SIGMOID)
+            return result
+
+        multiply(0, third, x0_blocks, codes[:, 0:P], scales[:, 0:P])
+        multiply(0, fourth, x0_blocks, codes[:, P:HALF], scales[:, P:HALF])
+        multiply(1, third, x1_blocks, *late_mx[0])
+        multiply(1, fourth, x1_blocks, *late_mx[1])
+        third_parts = first_step(third, "third")
+        fourth_parts = first_step(fourth, "fourth")
+        result_b = second_step(*third_parts, banks[0], banks[1], "result_b")
+        nc.sync.dma_start(out[HALF : HALF + P, :], result_b[:])
+        result_c = second_step(*fourth_parts, banks[7], banks[6], "result_c")
+        nc.sync.dma_start(out[HALF + P : DOCS, 0:HALF], result_c[:, 0:HALF])
+        nc.scalar.dma_start(out[HALF + P : DOCS, HALF:PICKED], result_c[:, HALF:PICKED])

@@ -117,7 +117,7 @@ def tile_picked_zplatt_sig_p_kernel(tc, x_words, x_scales, hT, gain, shift, offs
                     stop=b % per_bank == per_bank - 1 and o == 1,
                 )
 
-        early, third, fourth = ((0, 1, 2, 3), HALF, 1), ((3, 2), P, 2), ((4, 5), P, 2)
+        early, third, fourth = ((0, 1, 2, 3), HALF, 1), ((4, 5), P, 2), ((0, 1), P, 2)
         picked_rows = sb([P, PICKED], F32, "picked_rows", 48 * KIB)
         nc.vector.tensor_copy(picked_rows[:], row_window[:].indirect(offsets[:]))
         h0b_raw = load_docs(0, HALF, HALF, 10 * KIB)
@@ -146,7 +146,7 @@ def tile_picked_zplatt_sig_p_kernel(tc, x_words, x_scales, hT, gain, shift, offs
         multiply(0, early, x0_blocks, *quantise(h0a_grouped, "h0a"))
         h1a_mx = quantise(h1a_grouped, "h1a")
 
-        x1_blocks = sb([P, PICKED], U32, "x1_codes", 18 * KIB)
+        x1_blocks = sb([P, PICKED], U32, "x1_codes", 17 * KIB)
         for side in range(2):
             nc.vector.tensor_copy(
                 x1_blocks[:, HALF * side : HALF * (side + 1)],
@@ -160,14 +160,14 @@ def tile_picked_zplatt_sig_p_kernel(tc, x_words, x_scales, hT, gain, shift, offs
         def affine(target, source, b):
             nc.vector.tensor_scalar(target, source, platt[:, b, 0:1], platt[:, b, 1:2], MULT, ADD)
 
-        probs_a = sb([P, 4, HALF], F32, "probs_a")
-        for b in range(4):
+        h0b_grouped = sb([P, HALF, 4], BF16, "h0b_grouped", 19 * KIB)
+        probs_a = sb([P, 3, HALF], F32, "probs_a")
+        for b in range(3):
             squash(probs_a[:, b, :], sums(early, b), b)
 
-        h0b_grouped = sb([P, HALF, 4], BF16, "h0b_grouped", 40 * KIB)
         cast(nc.vector.tensor_copy, h0b_grouped[:], h0b_raw[:])
         codes, scales = quantise(h0b_grouped, "h0b")
-        late_grouped = [sb([P, P, 4], BF16, "late_grouped%d" % s, (40 + s) * KIB) for s in range(2)]
+        late_grouped = [sb([P, P, 4], BF16, "late_grouped%d" % s, (10 + s) * KIB) for s in range(2)]
         for s in range(2):
             cast(nc.vector.tensor_copy, late_grouped[s][:], late_raw[:, :, P * s : P * (s + 1)])
         late_mx = [quantise(late_grouped[s], "late%d" % s) for s in range(2)]
@@ -177,19 +177,16 @@ def tile_picked_zplatt_sig_p_kernel(tc, x_words, x_scales, hT, gain, shift, offs
                 nc.tensor.transpose(target[:, P * i : P * (i + 1)], sources[i], identity[:])
             return target[:, 0:HALF]
 
-        def early_pair(side, s):
-            return [probs_a[:, 2 * side + i, P * s : P * (s + 1)] for i in range(2)]
-
         early_rows = out[0:HALF, :].rearrange("(s p) l -> p s l", s=2)
-        early_left = sb([P, 2, HALF], F32, "early_left")
-        for s in range(2):
-            nc.scalar.copy(early_left[:, s, :], turn(banks[4 + s], early_pair(0, s)))
-        nc.sync.dma_start(early_rows[:, :, 0:HALF], early_left[:])
-        early_right = sb([P, 2, HALF], F32, "early_right")
-        for s in range(2):
-            turn(banks[6][:, HALF * s : HALF * (s + 1)], early_pair(1, s))
-        nc.scalar.copy(early_right[:], banks[6][:].rearrange("p (s l) -> p s l", s=2))
-        nc.sync.dma_start(early_rows[:, :, HALF:PICKED], early_right[:])
+        for b in range(3):
+            for s in range(2):
+                nc.tensor.transpose(banks[6 + s][:, P * b : P * (b + 1)], probs_a[:, b, P * s : P * (s + 1)], identity[:])
+        early_most = [sb([P, 3 * P], F32, "early_most0"), sb([P, 3 * P], F32, "early_most1", 10 * KIB - 256)]
+        for s, copy in enumerate((nc.scalar.copy, nc.vector.tensor_copy)):
+            copy(early_most[s][:], banks[6 + s][:, 0 : 3 * P])
+            nc.sync.dma_start(early_rows[:, s, 0 : 3 * P], early_most[s][:])
+        probs_last = sb([P, 2, P], F32, "probs_last", 11 * KIB + 512)
+        squash(probs_last[:].rearrange("p s d -> p (s d)"), sums(early, 3), 3)
 
         def first_step(chunk, name):
             left = sb([P, 2, P], F32, name + "_left")
@@ -213,8 +210,13 @@ def tile_picked_zplatt_sig_p_kernel(tc, x_words, x_scales, hT, gain, shift, offs
         multiply(1, fourth, x1_blocks, *late_mx[1])
         third_parts = first_step(third, "third")
         fourth_parts = first_step(fourth, "fourth")
-        result_b = second_step(*third_parts, banks[0], banks[1], "result_b")
+        early_rest = sb([P, 2, P], F32, "early_rest")
+        nc.vector.tensor_copy(
+            early_rest[:].rearrange("p s l -> p (s l)"), turn(banks[2], [probs_last[:, s, :] for s in range(2)])
+        )
+        nc.sync.dma_start(early_rows[:, :, 3 * P : PICKED], early_rest[:])
+        result_b = second_step(*third_parts, banks[6], banks[7], "result_b")
         nc.sync.dma_start(out[HALF : HALF + P, :], result_b[:])
-        result_c = second_step(*fourth_parts, banks[7], banks[6], "result_c")
+        result_c = second_step(*fourth_parts, banks[3], banks[4], "result_c")
         nc.sync.dma_start(out[HALF + P : DOCS, 0:HALF], result_c[:, 0:HALF])
         nc.scalar.dma_start(out[HALF + P : DOCS, HALF:PICKED], result_c[:, HALF:PICKED])

@@ -46,6 +46,8 @@ def tile_picked_zplatt_sig_p_kernel(tc, x_words, x_scales, hT, gain, shift, offs
         warm_out = sb([P, 1], F32, "warm_out")
         identity = sb([P, P], F32, "identity")
 
+        nc.scalar.dma_start(row_window[GAIN_ROW : GAIN_ROW + 1, :], gain[0:1, :])
+        nc.scalar.dma_start(row_window[GAIN_ROW + 1 : GAIN_ROW + 2, :], shift[0:1, :])
         nc.gpsimd.memset(warm_in[:], 0.0)
         nc.gpsimd.memset(scale_window[64:P, :].bitcast(I32), 0)
         nc.scalar.activation(warm_out[:], warm_in[:], SIGMOID)
@@ -66,8 +68,6 @@ def tile_picked_zplatt_sig_p_kernel(tc, x_words, x_scales, hT, gain, shift, offs
 
         nc.sync.dma_start(offsets[:], offs)
         nc.sync.dma_start(scale_window[0:SCALE_ROWS, :].bitcast(I32), x_scales.rearrange("o q n -> q o n").bitcast(I32))
-        nc.sync.dma_start(row_window[GAIN_ROW : GAIN_ROW + 1, :], gain[0:1, :])
-        nc.sync.dma_start(row_window[GAIN_ROW + 1 : GAIN_ROW + 2, :], shift[0:1, :])
         window0 = load_words(0, 18 * KIB)
         h0a_raw = load_docs(0, 0, HALF, 36 * KIB)
         h1a_raw = load_docs(1, 0, HALF)
@@ -118,7 +118,7 @@ def tile_picked_zplatt_sig_p_kernel(tc, x_words, x_scales, hT, gain, shift, offs
                 )
 
         early, third, fourth = ((0, 1, 2, 3), HALF, 1), ((4, 5), P, 2), ((0, 1), P, 2)
-        picked_rows = sb([P, PICKED], F32, "picked_rows", 48 * KIB)
+        picked_rows = sb([P, PICKED], F32, "picked_rows")
         nc.vector.tensor_copy(picked_rows[:], row_window[:].indirect(offsets[:]))
         h0b_raw = load_docs(0, HALF, HALF, 10 * KIB)
         for b in range(4):

@@ -127,16 +127,6 @@ def tile_picked_zplatt_sig_p_kernel(tc, x_words, x_scales, hT, gain, shift, offs
 
         x0_blocks = gather_words(window0, "x0_codes", 6 * KIB)
         late_raw = load_docs(1, HALF, HALF, 22 * KIB)
-        for b in range(2):
-            nc.tensor.matmul_mx(
-                out=banks[4][:],
-                lhsT=x0_blocks[:, 0:P].bitcast(FP8X4),
-                lhsT_scale=x_planes[:, 0, 0:P],
-                rhs=x0_blocks[:].bitcast(FP8X4),
-                rhs_scale=x_planes[:, 0, :],
-                start=True,
-                stop=True,
-            )
         h0a_grouped = sb([P, HALF, 4], BF16, "h0a_grouped")
         cast(nc.scalar.copy, h0a_grouped[:], h0a_raw[:])
         platt = sb([P, 4, 2], F32, "platt", 36 * KIB)
@@ -211,12 +201,13 @@ def tile_picked_zplatt_sig_p_kernel(tc, x_words, x_scales, hT, gain, shift, offs
         third_parts = first_step(third, "third")
         fourth_parts = first_step(fourth, "fourth")
         early_rest = sb([P, 2, P], F32, "early_rest")
-        nc.vector.tensor_copy(
+        nc.scalar.copy(
             early_rest[:].rearrange("p s l -> p (s l)"), turn(banks[2], [probs_last[:, s, :] for s in range(2)])
         )
         nc.sync.dma_start(early_rows[:, :, 3 * P : PICKED], early_rest[:])
         result_b = second_step(*third_parts, banks[6], banks[7], "result_b")
-        nc.sync.dma_start(out[HALF : HALF + P, :], result_b[:])
+        nc.sync.dma_start(out[HALF : HALF + P, 0:HALF], result_b[:, 0:HALF])
+        nc.sync.dma_start(out[HALF : HALF + P, HALF:PICKED], result_b[:, HALF:PICKED])
         result_c = second_step(*fourth_parts, banks[3], banks[4], "result_c")
         nc.sync.dma_start(out[HALF + P : DOCS, 0:HALF], result_c[:, 0:HALF])
         nc.scalar.dma_start(out[HALF + P : DOCS, HALF:PICKED], result_c[:, HALF:PICKED])

@@ -19,10 +19,26 @@ K, LABELS, PICKED, DOCS = 1024, 2048, 512, 512
 PASSES = 2
 FLOPS = 2 * K * PICKED * DOCS
 BYTES = K * LABELS + K // 32 * LABELS + 4 * K * DOCS + 2 * 4 * LABELS + 2 * PICKED + 4 * DOCS * PICKED
+HALF = 256
 GAIN_ROW = 126
 SCALE_ROWS = 32
-HALF = 256
+
 KIB = 1024
+ROW_WINDOW = 6 * KIB
+X0_CODES = ROW_WINDOW
+LATE0_RAW = ROW_WINDOW + 4 * KIB
+LATE1_GROUPED = LATE0_RAW
+TILE1_LEFT = LATE1_GROUPED + 256
+TILE1_RIGHT_PROBS = LATE1_GROUPED + KIB + 512
+WORD_WINDOW0 = 18 * KIB
+EARLY1_GROUPED = WORD_WINDOW0
+X1_CODES = EARLY1_GROUPED - KIB
+LATE0_GROUPED = EARLY1_GROUPED + KIB
+LATE1_RAW = WORD_WINDOW0 + 4 * KIB
+EARLY0_RAW = 36 * KIB
+PLATT = EARLY0_RAW
+WORD_WINDOW1 = 40 * KIB
+SCALE_WINDOW = WORD_WINDOW1 + 7 * KIB
 
 
 def tile_picked_zplatt_sig_p_kernel(tc, x_words, x_scales, hT, gain, shift, offs, out):
@@ -38,8 +54,8 @@ def tile_picked_zplatt_sig_p_kernel(tc, x_words, x_scales, hT, gain, shift, offs
             return reused.tile(shape, dtype, name=name, align_bytes=64, offset=at)
 
         offsets = sb([P, PICKED // 16], U16, "offsets")
-        scale_window = sb([P, LABELS], U8, "scale_window", 47 * KIB)
-        row_window = sb([P, LABELS], F32, "row_window", 6 * KIB)
+        scale_window = sb([P, LABELS], U8, "scale_window", SCALE_WINDOW)
+        row_window = sb([P, LABELS], F32, "row_window", ROW_WINDOW)
         x_planes = sb([P, PASSES, PICKED], U8, "x_planes")
         h_rows = [hT[512 * o : 512 * (o + 1), :].rearrange("(p j) t -> p j t", j=4) for o in range(PASSES)]
         warm_in = sb([P, 1], F32, "warm_in")
@@ -51,26 +67,26 @@ def tile_picked_zplatt_sig_p_kernel(tc, x_words, x_scales, hT, gain, shift, offs
         nc.gpsimd.memset(warm_in[:], 0.0)
         nc.gpsimd.memset(scale_window[64:P, :].bitcast(I32), 0)
         nc.scalar.activation(warm_out[:], warm_in[:], SIGMOID)
-        nc.vector.memset(scale_window[32:64, :].bitcast(I32), 0)
+        nc.vector.memset(scale_window[SCALE_ROWS:64, :].bitcast(I32), 0)
         nc.vector.memset(row_window[0:GAIN_ROW, :], 0.0)
         make_identity(nc, identity[:])
         nc.gpsimd.memset(x_planes[:].rearrange("p o s -> p (o s)").bitcast(I32), 0)
 
-        def load_words(o, at=None):
+        def load_words(o, at):
             window = sb([P, LABELS], I32, "word_window%d" % o, at)
             nc.sync.dma_start(window[:], x_words[o].rearrange("p n t -> p (n t)").bitcast(I32))
             return window
 
-        def load_docs(o, first, width, at=None):
-            raw = sb([P, 4, width], F32, "h%d_%d_raw" % (o, first), at)
-            nc.sync.dma_start(raw[:], h_rows[o][:, :, first : first + width])
+        def load_docs(o, first, at=None):
+            raw = sb([P, 4, HALF], F32, "h%d_%d_raw" % (o, first), at)
+            nc.sync.dma_start(raw[:], h_rows[o][:, :, first : first + HALF])
             return raw
 
         nc.sync.dma_start(offsets[:], offs)
         nc.sync.dma_start(scale_window[0:SCALE_ROWS, :].bitcast(I32), x_scales.rearrange("o q n -> q o n").bitcast(I32))
-        window0 = load_words(0, 18 * KIB)
-        h0a_raw = load_docs(0, 0, HALF, 36 * KIB)
-        h1a_raw = load_docs(1, 0, HALF)
+        window0 = load_words(0, WORD_WINDOW0)
+        early0_raw = load_docs(0, 0, EARLY0_RAW)
+        early1_raw = load_docs(1, 0)
 
         x_bytes = sb([P, PICKED], U8, "x_bytes")
         nc.vector.tensor_copy(x_bytes[:], scale_window[:].indirect(offsets[:]))
@@ -79,36 +95,33 @@ def tile_picked_zplatt_sig_p_kernel(tc, x_words, x_scales, hT, gain, shift, offs
                 x_planes[32 * q : 32 * q + 4].bitcast(I32),
                 x_bytes[8 * q : 8 * (q + 1), :].bitcast(I32),
             )
-        window1 = load_words(1, 40 * KIB)
+        window1 = load_words(1, WORD_WINDOW1)
 
         banks = [psum.tile([P, 512], F32, name="bank%d" % b) for b in range(8)]
-
-        def gather_words(window, name, at):
-            codes = sb([P, PICKED], U32, name, at)
-            nc.vector.tensor_copy(codes[:], window[:].bitcast(U32).indirect(offsets[:]))
-            return codes
 
         def cast(copy, grouped, raw):
             copy(grouped.rearrange("p (c i) j -> p c j i", i=4), raw.rearrange("p j (c i) -> p c j i", i=4))
 
-        def quantise(grouped, name, at=None):
+        def quantise(grouped, name):
             width = grouped.shape[1]
             codes = sb([P, width], U32, name + "_codes")
-            scales = sb([P, width], U8, name + "_scales", at)
+            scales = sb([P, width], U8, name + "_scales")
             nc.vector.quantize_mx(
                 out=codes[:].bitcast(FP8X4), scales=scales[:], in_=grouped[:].rearrange("p t j -> p (t j)")
             )
             return codes[:], scales[:]
 
-        def sums(chunk, b):
-            held, width, per_bank = chunk
+        early, tile2, tile3 = ((0, 1, 2, 3), HALF, 1), ((4, 5), P, 2), ((0, 1), P, 2)
+
+        def sums(group, b):
+            held, width, per_bank = group
             return banks[held[b // per_bank]][:, width * (b % per_bank) : width * (b % per_bank + 1)]
 
-        def multiply(o, chunk, label_codes, codes, scales):
-            per_bank = chunk[2]
+        def multiply(o, group, label_codes, codes, scales):
+            per_bank = group[2]
             for b in range(4):
                 nc.tensor.matmul_mx(
-                    out=sums(chunk, b),
+                    out=sums(group, b),
                     lhsT=label_codes[:, P * b : P * (b + 1)].bitcast(FP8X4),
                     lhsT_scale=x_planes[:, o, P * b : P * (b + 1)],
                     rhs=codes.bitcast(FP8X4),
@@ -117,32 +130,32 @@ def tile_picked_zplatt_sig_p_kernel(tc, x_words, x_scales, hT, gain, shift, offs
                     stop=b % per_bank == per_bank - 1 and o == 1,
                 )
 
-        early, third, fourth = ((0, 1, 2, 3), HALF, 1), ((4, 5), P, 2), ((0, 1), P, 2)
         picked_rows = sb([P, PICKED], F32, "picked_rows")
         nc.vector.tensor_copy(picked_rows[:], row_window[:].indirect(offsets[:]))
-        h0b_raw = load_docs(0, HALF, HALF, 10 * KIB)
+        late0_raw = load_docs(0, HALF, LATE0_RAW)
         for b in range(4):
             nc.tensor.transpose(banks[7][:, P * b : P * (b + 1)], picked_rows[:, P * b : P * (b + 1)], identity[:])
         turned_rows = banks[7][:].rearrange("p (b r) -> p b r", b=4)[:, :, GAIN_ROW : GAIN_ROW + 2]
 
-        x0_blocks = gather_words(window0, "x0_codes", 6 * KIB)
-        late_raw = load_docs(1, HALF, HALF, 22 * KIB)
-        h0a_grouped = sb([P, HALF, 4], BF16, "h0a_grouped")
-        cast(nc.scalar.copy, h0a_grouped[:], h0a_raw[:])
-        platt = sb([P, 4, 2], F32, "platt", 36 * KIB)
+        x0_codes = sb([P, PICKED], U32, "x0_codes", X0_CODES)
+        nc.vector.tensor_copy(x0_codes[:], window0[:].bitcast(U32).indirect(offsets[:]))
+        late1_raw = load_docs(1, HALF, LATE1_RAW)
+        early0_grouped = sb([P, HALF, 4], BF16, "early0_grouped")
+        cast(nc.scalar.copy, early0_grouped[:], early0_raw[:])
+        platt = sb([P, 4, 2], F32, "platt", PLATT)
         nc.scalar.copy(platt[:], turned_rows)
-        h1a_grouped = sb([P, HALF, 4], BF16, "h1a_grouped", 18 * KIB)
-        cast(nc.vector.tensor_copy, h1a_grouped[:], h1a_raw[:])
-        multiply(0, early, x0_blocks, *quantise(h0a_grouped, "h0a"))
-        h1a_mx = quantise(h1a_grouped, "h1a")
+        early1_grouped = sb([P, HALF, 4], BF16, "early1_grouped", EARLY1_GROUPED)
+        cast(nc.vector.tensor_copy, early1_grouped[:], early1_raw[:])
+        multiply(0, early, x0_codes, *quantise(early0_grouped, "early0"))
+        early1_mx = quantise(early1_grouped, "early1")
 
-        x1_blocks = sb([P, PICKED], U32, "x1_codes", 17 * KIB)
+        x1_codes = sb([P, PICKED], U32, "x1_codes", X1_CODES)
         for side in range(2):
             nc.vector.tensor_copy(
-                x1_blocks[:, HALF * side : HALF * (side + 1)],
+                x1_codes[:, HALF * side : HALF * (side + 1)],
                 window1[:].bitcast(U32).indirect(offsets[:, 16 * side : 16 * (side + 1)]),
             )
-        multiply(1, early, x1_blocks, *h1a_mx)
+        multiply(1, early, x1_codes, *early1_mx)
 
         def squash(target, source, b):
             nc.scalar.activation(target, source, SIGMOID, bias=platt[:, b, 1:2], scale=platt[:, b, 0:1])
@@ -150,40 +163,45 @@ def tile_picked_zplatt_sig_p_kernel(tc, x_words, x_scales, hT, gain, shift, offs
         def affine(target, source, b):
             nc.vector.tensor_scalar(target, source, platt[:, b, 0:1], platt[:, b, 1:2], MULT, ADD)
 
-        h0b_grouped = sb([P, HALF, 4], BF16, "h0b_grouped", 19 * KIB)
-        probs_a = sb([P, 3, HALF], F32, "probs_a")
-        for b in range(3):
-            squash(probs_a[:, b, :], sums(early, b), b)
+        late0_grouped = sb([P, HALF, 4], BF16, "late0_grouped", LATE0_GROUPED)
+        early_probs = sb([P, 3, HALF], F32, "early_probs")
+        for b in range(2):
+            squash(early_probs[:, b, :], sums(early, b), b)
+        for i in range(2):
+            squash(early_probs[:, 2, P * i : P * (i + 1)], sums(early, 2 + i)[:, 0:P], 2 + i)
 
-        cast(nc.vector.tensor_copy, h0b_grouped[:], h0b_raw[:])
-        codes, scales = quantise(h0b_grouped, "h0b")
-        late_grouped = [sb([P, P, 4], BF16, "late_grouped%d" % s, (10 + s) * KIB) for s in range(2)]
+        cast(nc.vector.tensor_copy, late0_grouped[:], late0_raw[:])
+        late0_codes, late0_scales = quantise(late0_grouped, "late0")
+        late1_grouped = [sb([P, P, 4], BF16, "late1_grouped%d" % s, LATE1_GROUPED + KIB * s) for s in range(2)]
         for s in range(2):
-            cast(nc.vector.tensor_copy, late_grouped[s][:], late_raw[:, :, P * s : P * (s + 1)])
-        late_mx = [quantise(late_grouped[s], "late%d" % s) for s in range(2)]
+            cast(nc.vector.tensor_copy, late1_grouped[s][:], late1_raw[:, :, P * s : P * (s + 1)])
+        late1_mx = [quantise(late1_grouped[s], "late1_%d" % s) for s in range(2)]
 
         def turn(target, sources):
             for i in range(2):
                 nc.tensor.transpose(target[:, P * i : P * (i + 1)], sources[i], identity[:])
             return target[:, 0:HALF]
 
-        early_rows = out[0:HALF, :].rearrange("(s p) l -> p s l", s=2)
-        for b in range(3):
+        for b in range(2):
             for s in range(2):
-                nc.tensor.transpose(banks[6 + s][:, P * b : P * (b + 1)], probs_a[:, b, P * s : P * (s + 1)], identity[:])
-        early_most = [sb([P, 3 * P], F32, "early_most0"), sb([P, 3 * P], F32, "early_most1", 10 * KIB - 256)]
-        for s, copy in enumerate((nc.scalar.copy, nc.vector.tensor_copy)):
-            copy(early_most[s][:], banks[6 + s][:, 0 : 3 * P])
-            nc.sync.dma_start(early_rows[:, s, 0 : 3 * P], early_most[s][:])
-        probs_last = sb([P, 2, P], F32, "probs_last", 11 * KIB + 512)
-        squash(probs_last[:].rearrange("p s d -> p (s d)"), sums(early, 3), 3)
+                nc.tensor.transpose(banks[6 + s][:, P * b : P * (b + 1)], early_probs[:, b, P * s : P * (s + 1)], identity[:])
+        turn(banks[6][:, HALF:PICKED], [early_probs[:, 2, P * i : P * (i + 1)] for i in range(2)])
+        tile0_result = sb([P, PICKED], F32, "tile0_result")
+        nc.scalar.copy(tile0_result[:], banks[6][:])
+        nc.sync.dma_start(out[0:P, :], tile0_result[:])
+        tile1_left = sb([P, HALF], F32, "tile1_left", TILE1_LEFT)
+        nc.vector.tensor_copy(tile1_left[:], banks[7][:, 0:HALF])
+        nc.sync.dma_start(out[P:HALF, 0:HALF], tile1_left[:])
+        tile1_right_probs = sb([P, 2, P], F32, "tile1_right_probs", TILE1_RIGHT_PROBS)
+        for i in range(2):
+            squash(tile1_right_probs[:, i, :], sums(early, 2 + i)[:, P:HALF], 2 + i)
 
-        def first_step(chunk, name):
+        def first_step(group, name):
             left = sb([P, 2, P], F32, name + "_left")
             right = sb([P, 2, P], F32, name + "_right")
             for i in range(2):
-                squash(left[:, i, :], sums(chunk, i), i)
-                affine(right[:, i, :], sums(chunk, 2 + i), 2 + i)
+                squash(left[:, i, :], sums(group, i), i)
+                affine(right[:, i, :], sums(group, 2 + i), 2 + i)
             return left, right
 
         def second_step(left, right, left_bank, right_bank, name):
@@ -194,20 +212,19 @@ def tile_picked_zplatt_sig_p_kernel(tc, x_words, x_scales, hT, gain, shift, offs
             nc.scalar.activation(result[:, HALF:PICKED], turned_right, SIGMOID)
             return result
 
-        multiply(0, third, x0_blocks, codes[:, 0:P], scales[:, 0:P])
-        multiply(0, fourth, x0_blocks, codes[:, P:HALF], scales[:, P:HALF])
-        multiply(1, third, x1_blocks, *late_mx[0])
-        multiply(1, fourth, x1_blocks, *late_mx[1])
-        third_parts = first_step(third, "third")
-        fourth_parts = first_step(fourth, "fourth")
-        early_rest = sb([P, 2, P], F32, "early_rest")
-        nc.scalar.copy(
-            early_rest[:].rearrange("p s l -> p (s l)"), turn(banks[2], [probs_last[:, s, :] for s in range(2)])
-        )
-        nc.sync.dma_start(early_rows[:, :, 3 * P : PICKED], early_rest[:])
-        result_b = second_step(*third_parts, banks[6], banks[7], "result_b")
-        nc.sync.dma_start(out[HALF : HALF + P, 0:HALF], result_b[:, 0:HALF])
-        nc.sync.dma_start(out[HALF : HALF + P, HALF:PICKED], result_b[:, HALF:PICKED])
-        result_c = second_step(*fourth_parts, banks[3], banks[4], "result_c")
-        nc.sync.dma_start(out[HALF + P : DOCS, 0:HALF], result_c[:, 0:HALF])
-        nc.scalar.dma_start(out[HALF + P : DOCS, HALF:PICKED], result_c[:, HALF:PICKED])
+        multiply(0, tile2, x0_codes, late0_codes[:, 0:P], late0_scales[:, 0:P])
+        multiply(0, tile3, x0_codes, late0_codes[:, P:HALF], late0_scales[:, P:HALF])
+        multiply(1, tile2, x1_codes, *late1_mx[0])
+        multiply(1, tile3, x1_codes, *late1_mx[1])
+        tile2_parts = first_step(tile2, "tile2")
+        tile3_parts = first_step(tile3, "tile3")
+        tile1_right = sb([P, HALF], F32, "tile1_right")
+        nc.scalar.copy(tile1_right[:], turn(banks[2], [tile1_right_probs[:, i, :] for i in range(2)]))
+        nc.sync.dma_start(out[P:HALF, HALF:PICKED], tile1_right[:])
+
+        tile2_result = second_step(*tile2_parts, banks[6], banks[7], "tile2_result")
+        nc.sync.dma_start(out[HALF : HALF + P, 0:HALF], tile2_result[:, 0:HALF])
+        nc.sync.dma_start(out[HALF : HALF + P, HALF:PICKED], tile2_result[:, HALF:PICKED])
+        tile3_result = second_step(*tile3_parts, banks[3], banks[4], "tile3_result")
+        nc.sync.dma_start(out[HALF + P : DOCS, 0:HALF], tile3_result[:, 0:HALF])
+        nc.scalar.dma_start(out[HALF + P : DOCS, HALF:PICKED], tile3_result[:, HALF:PICKED])

@@ -27,13 +27,11 @@ KIB = 1024
 ROW_WINDOW = 6 * KIB
 X0_CODES = ROW_WINDOW
 LATE0_RAW = ROW_WINDOW + 4 * KIB
-LATE1_GROUPED = LATE0_RAW
-TILE1_LEFT = LATE1_GROUPED + 256
-TILE1_RIGHT_PROBS = LATE1_GROUPED + KIB + 512
 WORD_WINDOW0 = 18 * KIB
 EARLY1_GROUPED = WORD_WINDOW0
-X1_CODES = EARLY1_GROUPED - KIB
-LATE0_GROUPED = EARLY1_GROUPED + KIB
+X1_CODES = EARLY1_GROUPED + 64 - 2 * KIB
+LATE_GROUPED = (EARLY1_GROUPED + 64 + KIB, EARLY1_GROUPED + 64)
+TILE1_LEFT = LATE_GROUPED[0]
 LATE1_RAW = WORD_WINDOW0 + 4 * KIB
 EARLY0_RAW = 36 * KIB
 PLATT = EARLY0_RAW
@@ -163,19 +161,24 @@ def tile_picked_zplatt_sig_p_kernel(tc, x_words, x_scales, hT, gain, shift, offs
         def affine(target, source, b):
             nc.vector.tensor_scalar(target, source, platt[:, b, 0:1], platt[:, b, 1:2], MULT, ADD)
 
-        late0_grouped = sb([P, HALF, 4], BF16, "late0_grouped", LATE0_GROUPED)
         early_probs = sb([P, 3, HALF], F32, "early_probs")
         for b in range(2):
             squash(early_probs[:, b, :], sums(early, b), b)
         for i in range(2):
             squash(early_probs[:, 2, P * i : P * (i + 1)], sums(early, 2 + i)[:, 0:P], 2 + i)
 
-        cast(nc.vector.tensor_copy, late0_grouped[:], late0_raw[:])
-        late0_codes, late0_scales = quantise(late0_grouped, "late0")
-        late1_grouped = [sb([P, P, 4], BF16, "late1_grouped%d" % s, LATE1_GROUPED + KIB * s) for s in range(2)]
-        for s in range(2):
-            cast(nc.vector.tensor_copy, late1_grouped[s][:], late1_raw[:, :, P * s : P * (s + 1)])
-        late1_mx = [quantise(late1_grouped[s], "late1_%d" % s) for s in range(2)]
+        tile1_right_probs = sb([P, 2, P], F32, "tile1_right_probs")
+        for i in range(2):
+            squash(tile1_right_probs[:, i, :], sums(early, 2 + i)[:, P:HALF], 2 + i)
+
+        def late_operands(o, raw):
+            grouped = [sb([P, P, 4], BF16, "late%d_grouped%d" % (o, s), LATE_GROUPED[s]) for s in range(2)]
+            for s in range(2):
+                cast(nc.vector.tensor_copy, grouped[s][:], raw[:, :, P * s : P * (s + 1)])
+            return [quantise(grouped[s], "late%d_%d" % (o, s)) for s in range(2)]
+
+        late0_mx = late_operands(0, late0_raw)
+        late1_mx = late_operands(1, late1_raw)
 
         def turn(target, sources):
             for i in range(2):
@@ -192,9 +195,6 @@ def tile_picked_zplatt_sig_p_kernel(tc, x_words, x_scales, hT, gain, shift, offs
         tile1_left = sb([P, HALF], F32, "tile1_left", TILE1_LEFT)
         nc.vector.tensor_copy(tile1_left[:], banks[7][:, 0:HALF])
         nc.sync.dma_start(out[P:HALF, 0:HALF], tile1_left[:])
-        tile1_right_probs = sb([P, 2, P], F32, "tile1_right_probs", TILE1_RIGHT_PROBS)
-        for i in range(2):
-            squash(tile1_right_probs[:, i, :], sums(early, 2 + i)[:, P:HALF], 2 + i)
 
         def first_step(group, name):
             left = sb([P, 2, P], F32, name + "_left")
@@ -212,19 +212,19 @@ def tile_picked_zplatt_sig_p_kernel(tc, x_words, x_scales, hT, gain, shift, offs
             nc.scalar.activation(result[:, HALF:PICKED], turned_right, SIGMOID)
             return result
 
-        multiply(0, tile2, x0_codes, late0_codes[:, 0:P], late0_scales[:, 0:P])
-        multiply(0, tile3, x0_codes, late0_codes[:, P:HALF], late0_scales[:, P:HALF])
+        multiply(0, tile2, x0_codes, *late0_mx[0])
+        multiply(0, tile3, x0_codes, *late0_mx[1])
         multiply(1, tile2, x1_codes, *late1_mx[0])
         multiply(1, tile3, x1_codes, *late1_mx[1])
         tile2_parts = first_step(tile2, "tile2")
         tile3_parts = first_step(tile3, "tile3")
         tile1_right = sb([P, HALF], F32, "tile1_right")
-        nc.scalar.copy(tile1_right[:], turn(banks[2], [tile1_right_probs[:, i, :] for i in range(2)]))
+        nc.scalar.copy(tile1_right[:], turn(banks[7][:, HALF:PICKED], [tile1_right_probs[:, i, :] for i in range(2)]))
         nc.sync.dma_start(out[P:HALF, HALF:PICKED], tile1_right[:])
 
-        tile2_result = second_step(*tile2_parts, banks[6], banks[7], "tile2_result")
+        tile2_result = second_step(*tile2_parts, banks[2], banks[3], "tile2_result")
         nc.sync.dma_start(out[HALF : HALF + P, 0:HALF], tile2_result[:, 0:HALF])
         nc.sync.dma_start(out[HALF : HALF + P, HALF:PICKED], tile2_result[:, HALF:PICKED])
-        tile3_result = second_step(*tile3_parts, banks[3], banks[4], "tile3_result")
+        tile3_result = second_step(*tile3_parts, banks[6], banks[4], "tile3_result")
         nc.sync.dma_start(out[HALF + P : DOCS, 0:HALF], tile3_result[:, 0:HALF])
         nc.scalar.dma_start(out[HALF + P : DOCS, HALF:PICKED], tile3_result[:, HALF:PICKED])

@@ -28,7 +28,8 @@ ROW_WINDOW = 6 * KIB
 X0_CODES = ROW_WINDOW
 LATE0_RAW = ROW_WINDOW + 4 * KIB
 WORD_WINDOW0 = 18 * KIB
-EARLY1_GROUPED = WORD_WINDOW0
+EARLY0_GROUPED = 30 * KIB
+EARLY1_GROUPED = EARLY0_GROUPED
 X1_CODES = EARLY1_GROUPED + 64 - 2 * KIB
 LATE_GROUPED = (EARLY1_GROUPED + 64 + KIB, EARLY1_GROUPED + 64)
 TILE1_LEFT = LATE_GROUPED[0]
@@ -138,14 +139,26 @@ def tile_picked_zplatt_sig_p_kernel(tc, x_words, x_scales, hT, gain, shift, offs
         x0_codes = sb([P, PICKED], U32, "x0_codes", X0_CODES)
         nc.vector.tensor_copy(x0_codes[:], window0[:].bitcast(U32).indirect(offsets[:]))
         late1_raw = load_docs(1, HALF, LATE1_RAW)
-        early0_grouped = sb([P, HALF, 4], BF16, "early0_grouped")
+        early0_grouped = sb([P, HALF, 4], BF16, "early0_grouped", EARLY0_GROUPED)
         cast(nc.scalar.copy, early0_grouped[:], early0_raw[:])
         platt = sb([P, 4, 2], F32, "platt", PLATT)
         nc.scalar.copy(platt[:], turned_rows)
+        early0_mx = quantise(early0_grouped, "early0")
+        multiply(0, early, x0_codes, *early0_mx)
         early1_grouped = sb([P, HALF, 4], BF16, "early1_grouped", EARLY1_GROUPED)
         cast(nc.vector.tensor_copy, early1_grouped[:], early1_raw[:])
-        multiply(0, early, x0_codes, *quantise(early0_grouped, "early0"))
         early1_mx = quantise(early1_grouped, "early1")
+
+        for s in range(2):
+            nc.tensor.matmul_mx(
+                out=banks[6][:],
+                lhsT=early0_mx[0][:, P * s : P * (s + 1)].bitcast(FP8X4),
+                lhsT_scale=early0_mx[1][:, P * s : P * (s + 1)],
+                rhs=x0_codes[:].bitcast(FP8X4),
+                rhs_scale=x_planes[:, 0, :],
+                start=True,
+                stop=True,
+            )
 
         x1_codes = sb([P, PICKED], U32, "x1_codes", X1_CODES)
         for side in range(2):

@@ -29,9 +29,9 @@ X0_CODES = ROW_WINDOW
 LATE0_RAW = ROW_WINDOW + 4 * KIB
 WORD_WINDOW0 = 18 * KIB
 EARLY0_GROUPED = 30 * KIB
-EARLY1_GROUPED = EARLY0_GROUPED
-X1_CODES = EARLY1_GROUPED + 64 - 2 * KIB
-LATE_GROUPED = (EARLY1_GROUPED + 64 + KIB, EARLY1_GROUPED + 64)
+EARLY1_GROUPED = WORD_WINDOW0
+X1_CODES = EARLY0_GROUPED + 64 - 2 * KIB
+LATE_GROUPED = (EARLY0_GROUPED + 64 + KIB, EARLY0_GROUPED + 64)
 TILE1_LEFT = LATE_GROUPED[0]
 LATE1_RAW = WORD_WINDOW0 + 4 * KIB
 EARLY0_RAW = 36 * KIB
@@ -84,8 +84,8 @@ def tile_picked_zplatt_sig_p_kernel(tc, x_words, x_scales, hT, gain, shift, offs
         nc.sync.dma_start(offsets[:], offs)
         nc.sync.dma_start(scale_window[0:SCALE_ROWS, :].bitcast(I32), x_scales.rearrange("o q n -> q o n").bitcast(I32))
         window0 = load_words(0, WORD_WINDOW0)
-        early0_raw = load_docs(0, 0, EARLY0_RAW)
         early1_raw = load_docs(1, 0)
+        early0_raw = load_docs(0, 0, EARLY0_RAW)
 
         x_bytes = sb([P, PICKED], U8, "x_bytes")
         nc.vector.tensor_copy(x_bytes[:], scale_window[:].indirect(offsets[:]))
@@ -139,26 +139,25 @@ def tile_picked_zplatt_sig_p_kernel(tc, x_words, x_scales, hT, gain, shift, offs
         x0_codes = sb([P, PICKED], U32, "x0_codes", X0_CODES)
         nc.vector.tensor_copy(x0_codes[:], window0[:].bitcast(U32).indirect(offsets[:]))
         late1_raw = load_docs(1, HALF, LATE1_RAW)
+        early1_grouped = sb([P, HALF, 4], BF16, "early1_grouped", EARLY1_GROUPED)
+        cast(nc.vector.tensor_copy, early1_grouped[:], early1_raw[:])
+        early1_mx = quantise(early1_grouped, "early1")
         early0_grouped = sb([P, HALF, 4], BF16, "early0_grouped", EARLY0_GROUPED)
         cast(nc.scalar.copy, early0_grouped[:], early0_raw[:])
         platt = sb([P, 4, 2], F32, "platt", PLATT)
         nc.scalar.copy(platt[:], turned_rows)
-        early0_mx = quantise(early0_grouped, "early0")
-        multiply(0, early, x0_codes, *early0_mx)
-        early1_grouped = sb([P, HALF, 4], BF16, "early1_grouped", EARLY1_GROUPED)
-        cast(nc.vector.tensor_copy, early1_grouped[:], early1_raw[:])
-        early1_mx = quantise(early1_grouped, "early1")
-
-        for s in range(2):
+        for width in (HALF, P):
             nc.tensor.matmul_mx(
-                out=banks[6][:],
-                lhsT=early0_mx[0][:, P * s : P * (s + 1)].bitcast(FP8X4),
-                lhsT_scale=early0_mx[1][:, P * s : P * (s + 1)],
-                rhs=x0_codes[:].bitcast(FP8X4),
-                rhs_scale=x_planes[:, 0, :],
+                out=banks[7][:, 0:width],
+                lhsT=early1_mx[0][:, 0:P].bitcast(FP8X4),
+                lhsT_scale=early1_mx[1][:, 0:P],
+                rhs=x0_codes[:, 0:width].bitcast(FP8X4),
+                rhs_scale=x_planes[:, 0, 0:width],
                 start=True,
                 stop=True,
             )
+        early0_mx = quantise(early0_grouped, "early0")
+        multiply(0, early, x0_codes, *early0_mx)
 
         x1_codes = sb([P, PICKED], U32, "x1_codes", X1_CODES)
         for side in range(2):

@@ -21,6 +21,7 @@ FLOPS = 2 * K * PICKED * DOCS
 BYTES = K * LABELS + K // 32 * LABELS + 4 * K * DOCS + 2 * 4 * LABELS + 2 * PICKED + 4 * DOCS * PICKED
 HALF = 256
 GAIN_ROW = 126
+SCALAR_DOCS = 192
 SCALE_ROWS = 32
 
 KIB = 1024
@@ -143,29 +144,33 @@ def tile_picked_zplatt_sig_p_kernel(tc, x_words, x_scales, hT, gain, shift, offs
         cast(nc.vector.tensor_copy, early1_grouped[:], early1_raw[:])
         early1_mx = quantise(early1_grouped, "early1")
         early0_grouped = sb([P, HALF, 4], BF16, "early0_grouped", EARLY0_GROUPED)
-        cast(nc.scalar.copy, early0_grouped[:], early0_raw[:])
+        cast(nc.vector.tensor_copy, early0_grouped[:, SCALAR_DOCS:HALF, :], early0_raw[:, :, SCALAR_DOCS:HALF])
+        cast(nc.scalar.copy, early0_grouped[:, 0:SCALAR_DOCS, :], early0_raw[:, :, 0:SCALAR_DOCS])
         platt = sb([P, 4, 2], F32, "platt", PLATT)
         nc.scalar.copy(platt[:], turned_rows)
-        for width in (HALF, P):
+        def warm_up(o, label_codes, first, last):
             nc.tensor.matmul_mx(
-                out=banks[7][:, 0:width],
+                out=banks[7][:, 0 : last - first],
                 lhsT=early1_mx[0][:, 0:P].bitcast(FP8X4),
                 lhsT_scale=early1_mx[1][:, 0:P],
-                rhs=x0_codes[:, 0:width].bitcast(FP8X4),
-                rhs_scale=x_planes[:, 0, 0:width],
+                rhs=label_codes[:, first:last].bitcast(FP8X4),
+                rhs_scale=x_planes[:, o, first:last],
                 start=True,
                 stop=True,
             )
+
+        warm_up(0, x0_codes, 0, P)
         early0_mx = quantise(early0_grouped, "early0")
         multiply(0, early, x0_codes, *early0_mx)
 
         x1_codes = sb([P, PICKED], U32, "x1_codes", X1_CODES)
-        for side in range(2):
+        for b in range(4):
             nc.vector.tensor_copy(
-                x1_codes[:, HALF * side : HALF * (side + 1)],
-                window1[:].bitcast(U32).indirect(offsets[:, 16 * side : 16 * (side + 1)]),
+                x1_codes[:, P * b : P * (b + 1)],
+                window1[:].bitcast(U32).indirect(offsets[:, 8 * b : 8 * (b + 1)]),
             )
         multiply(1, early, x1_codes, *early1_mx)
+        warm_up(1, x1_codes, HALF, PICKED)
 
         def squash(target, source, b):
             nc.scalar.activation(target, source, SIGMOID, bias=platt[:, b, 1:2], scale=platt[:, b, 0:1])

@@ -148,18 +148,6 @@ def tile_picked_zplatt_sig_p_kernel(tc, x_words, x_scales, hT, gain, shift, offs
         cast(nc.scalar.copy, early0_grouped[:, 0:SCALAR_DOCS, :], early0_raw[:, :, 0:SCALAR_DOCS])
         platt = sb([P, 4, 2], F32, "platt", PLATT)
         nc.scalar.copy(platt[:], turned_rows)
-        def warm_up(o, label_codes, first, last):
-            nc.tensor.matmul_mx(
-                out=banks[7][:, 0 : last - first],
-                lhsT=early1_mx[0][:, 0:P].bitcast(FP8X4),
-                lhsT_scale=early1_mx[1][:, 0:P],
-                rhs=label_codes[:, first:last].bitcast(FP8X4),
-                rhs_scale=x_planes[:, o, first:last],
-                start=True,
-                stop=True,
-            )
-
-        warm_up(0, x0_codes, 0, P)
         early0_mx = quantise(early0_grouped, "early0")
         multiply(0, early, x0_codes, *early0_mx)
 
@@ -170,7 +158,6 @@ def tile_picked_zplatt_sig_p_kernel(tc, x_words, x_scales, hT, gain, shift, offs
                 window1[:].bitcast(U32).indirect(offsets[:, 8 * b : 8 * (b + 1)]),
             )
         multiply(1, early, x1_codes, *early1_mx)
-        warm_up(1, x1_codes, HALF, PICKED)
 
         def squash(target, source, b):
             nc.scalar.activation(target, source, SIGMOID, bias=platt[:, b, 1:2], scale=platt[:, b, 0:1])

from contextlib import ExitStack

import concourse.mybir as mybir
from concourse.masks import make_identity

F32 = mybir.dt.float32
BF16 = mybir.dt.bfloat16
I32 = mybir.dt.int32
U32 = mybir.dt.uint32
U16 = mybir.dt.uint16
U8 = mybir.dt.uint8
FP8X4 = mybir.dt.float8_e4m3fn_x4
SIGMOID = mybir.ActivationFunctionType.Sigmoid
MULT = mybir.AluOpType.mult
ADD = mybir.AluOpType.add

P = 128
K, LABELS, PICKED, DOCS = 1024, 2048, 512, 512
PASSES = 2
FLOPS = 2 * K * PICKED * DOCS
BYTES = K * LABELS + K // 32 * LABELS + 4 * K * DOCS + 2 * 4 * LABELS + 2 * PICKED + 4 * DOCS * PICKED
HALF = 256
GAIN_ROW = 126
SCALAR_DOCS = 192
SCALE_ROWS = 32

KIB = 1024
ROW_WINDOW = 6 * KIB
X0_CODES = ROW_WINDOW
LATE0_RAW = ROW_WINDOW + 4 * KIB
WORD_WINDOW0 = 18 * KIB
EARLY0_GROUPED = 30 * KIB
EARLY1_GROUPED = WORD_WINDOW0
X1_CODES = EARLY0_GROUPED + 64 - 2 * KIB
LATE_GROUPED = (EARLY0_GROUPED + 64 + KIB, EARLY0_GROUPED + 64)
TILE1_LEFT = LATE_GROUPED[0]
LATE1_RAW = WORD_WINDOW0 + 4 * KIB
EARLY0_RAW = 36 * KIB
PLATT = EARLY0_RAW
WORD_WINDOW1 = 40 * KIB
SCALE_WINDOW = WORD_WINDOW1 + 7 * KIB


def tile_picked_zplatt_sig_p_kernel(tc, x_words, x_scales, hT, gain, shift, offs, out):
    nc = tc.nc
    with ExitStack() as ctx:
        keep = ctx.enter_context(tc.tile_pool(name="keep", bufs=1))
        reused = ctx.enter_context(tc.tile_pool(name="reused", bufs=1))
        psum = ctx.enter_context(tc.psum_pool(name="psum", bufs=1))

        def sb(shape, dtype, name, at=None):
            if at is None:
                return keep.tile(shape, dtype, name=name, align_bytes=64)
            return reused.tile(shape, dtype, name=name, align_bytes=64, offset=at)

        offsets = sb([P, PICKED // 16], U16, "offsets")
        scale_window = sb([P, LABELS], U8, "scale_window", SCALE_WINDOW)
        row_window = sb([P, LABELS], F32, "row_window", ROW_WINDOW)
        x_planes = sb([P, PASSES, PICKED], U8, "x_planes")
        h_rows = [hT[512 * o : 512 * (o + 1), :].rearrange("(p j) t -> p j t", j=4) for o in range(PASSES)]
        warm_in = sb([P, 1], F32, "warm_in")
        warm_out = sb([P, 1], F32, "warm_out")
        identity = sb([P, P], F32, "identity")

        nc.scalar.dma_start(row_window[GAIN_ROW : GAIN_ROW + 1, :], gain[0:1, :])
        nc.scalar.dma_start(row_window[GAIN_ROW + 1 : GAIN_ROW + 2, :], shift[0:1, :])
        nc.gpsimd.memset(warm_in[:], 0.0)
        nc.gpsimd.memset(scale_window[64:P, :].bitcast(I32), 0)
        nc.scalar.activation(warm_out[:], warm_in[:], SIGMOID)
        nc.vector.memset(scale_window[SCALE_ROWS:64, :].bitcast(I32), 0)
        nc.vector.memset(row_window[0:GAIN_ROW, :], 0.0)
        make_identity(nc, identity[:])
        nc.gpsimd.memset(x_planes[:].rearrange("p o s -> p (o s)").bitcast(I32), 0)

        def load_words(o, at):
            window = sb([P, LABELS], I32, "word_window%d" % o, at)
            nc.sync.dma_start(window[:], x_words[o].rearrange("p n t -> p (n t)").bitcast(I32))
            return window

        def load_docs(o, first, at=None):
            raw = sb([P, 4, HALF], F32, "h%d_%d_raw" % (o, first), at)
            nc.sync.dma_start(raw[:], h_rows[o][:, :, first : first + HALF])
            return raw

        nc.sync.dma_start(offsets[:], offs)
        nc.sync.dma_start(scale_window[0:SCALE_ROWS, :].bitcast(I32), x_scales.rearrange("o q n -> q o n").bitcast(I32))
        window0 = load_words(0, WORD_WINDOW0)
        early1_raw = load_docs(1, 0)
        early0_raw = load_docs(0, 0, EARLY0_RAW)

        x_bytes = sb([P, PICKED], U8, "x_bytes")
        nc.vector.tensor_copy(x_bytes[:], scale_window[:].indirect(offsets[:]))
        for q in range(4):
            nc.sync.dma_start(
                x_planes[32 * q : 32 * q + 4].bitcast(I32),
                x_bytes[8 * q : 8 * (q + 1), :].bitcast(I32),
            )
        window1 = load_words(1, WORD_WINDOW1)

        banks = [psum.tile([P, 512], F32, name="bank%d" % b) for b in range(8)]

        def cast(copy, grouped, raw):
            copy(grouped.rearrange("p (c i) j -> p c j i", i=4), raw.rearrange("p j (c i) -> p c j i", i=4))

        def quantise(grouped, name):
            width = grouped.shape[1]
            codes = sb([P, width], U32, name + "_codes")
            scales = sb([P, width], U8, name + "_scales")
            nc.vector.quantize_mx(
                out=codes[:].bitcast(FP8X4), scales=scales[:], in_=grouped[:].rearrange("p t j -> p (t j)")
            )
            return codes[:], scales[:]

        early, tile2, tile3 = ((0, 1, 2, 3), HALF, 1), ((4, 5), P, 2), ((0, 1), P, 2)

        def sums(group, b):
            held, width, per_bank = group
            return banks[held[b // per_bank]][:, width * (b % per_bank) : width * (b % per_bank + 1)]

        def multiply(o, group, label_codes, codes, scales):
            per_bank = group[2]
            for b in range(4):
                nc.tensor.matmul_mx(
                    out=sums(group, b),
                    lhsT=label_codes[:, P * b : P * (b + 1)].bitcast(FP8X4),
                    lhsT_scale=x_planes[:, o, P * b : P * (b + 1)],
                    rhs=codes.bitcast(FP8X4),
                    rhs_scale=scales,
                    start=b % per_bank == 0 and o == 0,
                    stop=b % per_bank == per_bank - 1 and o == 1,
                )

        picked_rows = sb([P, PICKED], F32, "picked_rows")
        nc.vector.tensor_copy(picked_rows[:], row_window[:].indirect(offsets[:]))
        late0_raw = load_docs(0, HALF, LATE0_RAW)
        for b in range(4):
            nc.tensor.transpose(banks[7][:, P * b : P * (b + 1)], picked_rows[:, P * b : P * (b + 1)], identity[:])
        turned_rows = banks[7][:].rearrange("p (b r) -> p b r", b=4)[:, :, GAIN_ROW : GAIN_ROW + 2]

        x0_codes = sb([P, PICKED], U32, "x0_codes", X0_CODES)
        nc.vector.tensor_copy(x0_codes[:], window0[:].bitcast(U32).indirect(offsets[:]))
        late1_raw = load_docs(1, HALF, LATE1_RAW)
        early1_grouped = sb([P, HALF, 4], BF16, "early1_grouped", EARLY1_GROUPED)
        cast(nc.vector.tensor_copy, early1_grouped[:], early1_raw[:])
        early1_mx = quantise(early1_grouped, "early1")
        early0_grouped = sb([P, HALF, 4], BF16, "early0_grouped", EARLY0_GROUPED)
        cast(nc.vector.tensor_copy, early0_grouped[:, SCALAR_DOCS:HALF, :], early0_raw[:, :, SCALAR_DOCS:HALF])
        cast(nc.scalar.copy, early0_grouped[:, 0:SCALAR_DOCS, :], early0_raw[:, :, 0:SCALAR_DOCS])
        platt = sb([P, 4, 2], F32, "platt", PLATT)
        nc.scalar.copy(platt[:], turned_rows)
        early0_mx = quantise(early0_grouped, "early0")
        multiply(0, early, x0_codes, *early0_mx)

        x1_codes = sb([P, PICKED], U32, "x1_codes", X1_CODES)
        for b in range(4):
            nc.vector.tensor_copy(
                x1_codes[:, P * b : P * (b + 1)],
                window1[:].bitcast(U32).indirect(offsets[:, 8 * b : 8 * (b + 1)]),
            )
        multiply(1, early, x1_codes, *early1_mx)

        def squash(target, source, b):
            nc.scalar.activation(target, source, SIGMOID, bias=platt[:, b, 1:2], scale=platt[:, b, 0:1])

        def affine(target, source, b):
            nc.vector.tensor_scalar(target, source, platt[:, b, 0:1], platt[:, b, 1:2], MULT, ADD)

        early_probs = sb([P, 3, HALF], F32, "early_probs")
        for b in range(2):
            squash(early_probs[:, b, :], sums(early, b), b)
        for i in range(2):
            squash(early_probs[:, 2, P * i : P * (i + 1)], sums(early, 2 + i)[:, 0:P], 2 + i)

        tile1_right_probs = sb([P, 2, P], F32, "tile1_right_probs")
        for i in range(2):
            squash(tile1_right_probs[:, i, :], sums(early, 2 + i)[:, P:HALF], 2 + i)

        def late_operands(o, raw):
            grouped = [sb([P, P, 4], BF16, "late%d_grouped%d" % (o, s), LATE_GROUPED[s]) for s in range(2)]
            for s in range(2):
                cast(nc.vector.tensor_copy, grouped[s][:], raw[:, :, P * s : P * (s + 1)])
            return [quantise(grouped[s], "late%d_%d" % (o, s)) for s in range(2)]

        late0_mx = late_operands(0, late0_raw)
        late1_mx = late_operands(1, late1_raw)

        def turn(target, sources):
            for i in range(2):
                nc.tensor.transpose(target[:, P * i : P * (i + 1)], sources[i], identity[:])
            return target[:, 0:HALF]

        for b in range(2):
            for s in range(2):
                nc.tensor.transpose(banks[6 + s][:, P * b : P * (b + 1)], early_probs[:, b, P * s : P * (s + 1)], identity[:])
        turn(banks[6][:, HALF:PICKED], [early_probs[:, 2, P * i : P * (i + 1)] for i in range(2)])
        tile0_result = sb([P, PICKED], F32, "tile0_result")
        nc.scalar.copy(tile0_result[:], banks[6][:])
        nc.sync.dma_start(out[0:P, :], tile0_result[:])
        tile1_left = sb([P, HALF], F32, "tile1_left", TILE1_LEFT)
        nc.vector.tensor_copy(tile1_left[:], banks[7][:, 0:HALF])
        nc.sync.dma_start(out[P:HALF, 0:HALF], tile1_left[:])

        def first_step(group, name):
            left = sb([P, 2, P], F32, name + "_left")
            right = sb([P, 2, P], F32, name + "_right")
            for i in range(2):
                squash(left[:, i, :], sums(group, i), i)
                affine(right[:, i, :], sums(group, 2 + i), 2 + i)
            return left, right

        def second_step(left, right, left_bank, right_bank, name):
            result = sb([P, PICKED], F32, name)
            turned_left = turn(left_bank, [left[:, i, :] for i in range(2)])
            turned_right = turn(right_bank, [right[:, i, :] for i in range(2)])
            nc.vector.tensor_copy(result[:, 0:HALF], turned_left)
            nc.scalar.activation(result[:, HALF:PICKED], turned_right, SIGMOID)
            return result

        multiply(0, tile2, x0_codes, *late0_mx[0])
        multiply(0, tile3, x0_codes, *late0_mx[1])
        multiply(1, tile2, x1_codes, *late1_mx[0])
        multiply(1, tile3, x1_codes, *late1_mx[1])
        tile2_parts = first_step(tile2, "tile2")
        tile3_parts = first_step(tile3, "tile3")
        tile1_right = sb([P, HALF], F32, "tile1_right")
        nc.scalar.copy(tile1_right[:], turn(banks[7][:, HALF:PICKED], [tile1_right_probs[:, i, :] for i in range(2)]))
        nc.sync.dma_start(out[P:HALF, HALF:PICKED], tile1_right[:])

        tile2_result = second_step(*tile2_parts, banks[2], banks[3], "tile2_result")
        nc.sync.dma_start(out[HALF : HALF + P, 0:HALF], tile2_result[:, 0:HALF])
        nc.sync.dma_start(out[HALF : HALF + P, HALF:PICKED], tile2_result[:, HALF:PICKED])
        tile3_result = second_step(*tile3_parts, banks[6], banks[4], "tile3_result")
        nc.sync.dma_start(out[HALF + P : DOCS, 0:HALF], tile3_result[:, 0:HALF])
        nc.scalar.dma_start(out[HALF + P : DOCS, HALF:PICKED], tile3_result[:, HALF:PICKED])
